import numpy as np
import ml_dtypes


def mxq(x, axis, fmt="e4m3"):
    dtype, down = {"e4m3": (ml_dtypes.float8_e4m3fn, 7), "e5m2": (ml_dtypes.float8_e5m2, 14)}[fmt]
    v = np.moveaxis(np.asarray(x, np.float32).astype(ml_dtypes.bfloat16).astype(np.float64), axis, -1)
    blocks = v.reshape(v.shape[:-1] + (-1, 32))
    amax = np.abs(blocks).max(-1, keepdims=True)
    byte = np.maximum(np.where(amax > 0, np.frexp(amax)[1] - 1 + 127, 0) - down, 1)
    scale = np.exp2(byte - 127.0)
    codes = (blocks / scale).astype(np.float32).astype(dtype).astype(np.float64)
    return np.moveaxis((codes * scale).reshape(v.shape), -1, axis)


WIDE = False


def mx_kscale(k):
    if not WIDE:
        return np.ones(k)
    levels = np.array([10, -10, 5, -5, 0])
    if k % 512:
        return np.exp2(np.random.permutation(np.resize(levels, k // 32))).repeat(32)
    a = np.empty((k // 512, 16))
    for p in range(k // 512):
        a[p, :8] = np.random.permutation(np.resize(levels, 8))
        for g in range(8):
            far = levels[np.abs(levels - a[p, g]) >= 10]
            a[p, g + 8] = far[np.random.randint(len(far))]
    return np.exp2(a.ravel()).repeat(32)


def f64(x):
    return np.asarray(x).astype(np.float64)


def striped(idx):
    return np.tile(idx.reshape(-1, 16).T, (8, 1)).astype(np.uint16)


def unstriped(offs):
    return offs[:16].T.reshape(-1).astype(np.int64)


E2M1 = np.array([0.0, 0.5, 1.0, 1.5, 2.0, 3.0, 4.0, 6.0, -0.0, -0.5, -1.0, -1.5, -2.0, -3.0, -4.0, -6.0])


def pack_weight(w, fmt):
    k, n = w.shape
    w = f64(np.asarray(w, np.float32).astype(ml_dtypes.bfloat16)).reshape(k // 32, 32, n)
    amax = np.abs(w).max(1)
    if fmt == "e4m3":
        byte = np.frexp(amax)[1] - 1 + 127 - 7
    else:
        mant, ex = np.frexp(amax / 6.0)
        byte = np.where(mant > 0.5, ex, ex - 1) + 127
    byte = np.clip(np.where(amax > 0, byte, 1), 1, 254)
    scaled = (w * np.exp2(127.0 - byte)[:, None, :]).reshape(k, n).astype(np.float32)
    by_word = np.ascontiguousarray(scaled.reshape(k // 512, 128, 4, n).transpose(0, 1, 3, 2))
    if fmt == "e4m3":
        words = by_word.astype(ml_dtypes.float8_e4m3fn).view(np.uint8)
    else:
        c = by_word.astype(ml_dtypes.float4_e2m1fn).view(np.uint8) & 0xF
        words = (c[..., 0::2] | (c[..., 1::2] << 4)).reshape(k // 512, 128, 2 * n)
    return np.ascontiguousarray(words), np.ascontiguousarray(byte.astype(np.uint8).reshape(k // 512, 16, n))


def unpack_weight(words, scales, fmt):
    g, _, n = scales.shape
    words = np.ascontiguousarray(words).reshape(g, 128, n, -1)
    if fmt == "e4m3":
        vals = words.view(ml_dtypes.float8_e4m3fn).astype(np.float64)
    else:
        nib = np.empty((g, 128, n, 4), np.uint8)
        nib[..., 0::2] = words & 0xF
        nib[..., 1::2] = words >> 4
        vals = E2M1[nib]
    vals = vals * np.repeat(np.exp2(scales.astype(np.float64) - 127.0), 8, axis=1)[..., None]
    return vals.transpose(0, 1, 3, 2).reshape(g * 512, n)


def gelu(v):
    return 0.5 * v * (1.0 + np.tanh(np.sqrt(2.0 / np.pi) * (v + 0.044715 * v**3)))


def bf(x):
    return np.asarray(x, np.float32).astype(ml_dtypes.bfloat16)

def planes(Y):
    n, m = Y.shape
    b = f64(bf(Y)).reshape(n // 32, 32, m)
    amax = np.abs(b).max(1)
    byte = np.clip(np.where(amax > 0, np.frexp(amax)[1] - 1 + 127 - 7, 1), 1, 254)
    codes = (b * np.exp2(127.0 - byte)[:, None, :]).reshape(n, m).astype(np.float32).astype(ml_dtypes.float8_e4m3fn).view(np.uint8)
    words = codes.reshape(n // 512, 128, 4, m).transpose(0, 1, 3, 2)
    return np.ascontiguousarray(words), np.ascontiguousarray(byte.astype(np.uint8).reshape(n // 512, 16, m))


K, H, T, S = 512, 1024, 2048, 1024

def setup_inputs():
    n = np.random.standard_normal
    s = mx_kscale(K)[:, None]
    u = mx_kscale(H)[:, None]
    tab_words, tab_scales = pack_weight(n((K, T)) * s, "e4m3")
    wr_words, wr_scales = pack_weight(1.5 * n((K, H)) / np.sqrt(K) / s, "e2m1")
    uc_words, uc_scales = pack_weight(1.2 * n((H, H)) / np.sqrt(H) / u, "e4m3")
    return {
        "tab_words": tab_words, "tab_scales": tab_scales,
        "offs": striped(np.random.permutation(T)[:S]),
        "gT": (n((H, T)) * u).astype(np.float32),
        "wr_words": wr_words, "wr_scales": wr_scales,
        "wc": (0.8 * n((K, H)) / np.sqrt(K) / s).astype(np.float32),
        "uc_words": uc_words, "uc_scales": uc_scales,
        "b": (0.3 * n(H)).astype(np.float32),
        "gain": np.exp(0.8 * n(H)).astype(np.float32),
    }

def reference(tab_words, tab_scales, offs, gT, wr_words, wr_scales, wc, uc_words, uc_scales, b, gain):
    v = unpack_weight(tab_words, tab_scales, "e4m3")[:, unstriped(offs)]
    g = f64(gT)[:, unstriped(offs)]
    wr = unpack_weight(wr_words, wr_scales, "e2m1")
    uc = unpack_weight(uc_words, uc_scales, "e4m3")
    wcq = mxq(f64(wc), 0, "e4m3")
    a = wr.T @ v
    h = g / (1.0 + np.exp(-a))
    hq = mxq(h, 0, "e4m3")
    c = uc.T @ hq + wcq.T @ v
    y = np.tanh(c + f64(b)[:, None]) * f64(gain)[:, None]
    words, scales = planes(y)
    return y, words, scales

@@ -1,0 +1,238 @@
+from contextlib import ExitStack
+
+import concourse.mybir as mybir
+
+K, H, T, S = 512, 1024, 2048, 1024
+FLOPS = 2 * S * H * (2 * K + H)
+
+F32 = mybir.dt.float32
+BF16 = mybir.dt.bfloat16
+I32 = mybir.dt.int32
+U32 = mybir.dt.uint32
+U16 = mybir.dt.uint16
+U8 = mybir.dt.uint8
+FP8X4 = mybir.dt.float8_e4m3fn_x4
+FP4X4 = mybir.dt.float4_e2m1fn_x4
+ACT = mybir.ActivationFunctionType
+MULT = mybir.AluOpType.mult
+
+P = 128
+PACK = 4
+GROUP = P * PACK
+GROUPS = H // GROUP
+QUADS = 4
+RUN = 4
+SLICES = ((0, 256), (256, 512), (768, 256))
+WIDEST = 512
+
+
+def tile_list_gru_token_candidate_kernel(
+    tc, tab_words, tab_scales, offs, gT, wr_words, wr_scales, wc, uc_words, uc_scales, b, gain, out_0, out_1, out_2
+):
+    nc = tc.nc
+    with ExitStack() as ctx:
+        keep = ctx.enter_context(tc.tile_pool(name="keep", bufs=1))
+        ring = ctx.enter_context(tc.tile_pool(name="ring", bufs=2))
+        psum = ctx.enter_context(tc.psum_pool(name="psum", bufs=8))
+
+        offsets = keep.tile([P, S // 16], U16, name="offsets")
+        nc.sync.dma_start(offsets[:], offs)
+
+        wr_raw = keep.tile([P, 2 * H], U8, name="wr_raw", align_bytes=64)
+        nc.sync.dma_start(wr_raw[:].bitcast(I32), wr_words[0].bitcast(I32))
+        tab_w = keep.tile([P, T], I32, name="tab_w", align_bytes=64)
+        nc.sync.dma_start(tab_w[:], tab_words[0].rearrange("p t i -> p (t i)").bitcast(I32))
+        tab_s = keep.tile([P, T], U8, name="tab_s", align_bytes=64)
+        nc.gpsimd.memset(tab_s[:].bitcast(I32), 0)
+        for q in range(QUADS):
+            nc.sync.dma_start(tab_s[32 * q : 32 * q + 4, :].bitcast(I32), tab_scales[0, 4 * q : 4 * q + 4, :].bitcast(I32))
+
+        wr_w = keep.tile([P, 2 * H], U8, name="wr_w", align_bytes=64)
+        nc.vector.tensor_copy(
+            out=wr_w[:].bitcast(U16).rearrange("p (t c i) -> p c t i", t=PACK, i=8),
+            in_=wr_raw[:].bitcast(U16).rearrange("p (c i t) -> p c t i", t=PACK, i=8),
+        )
+        w_s_raw = keep.tile([P, H], U8, name="w_s_raw", align_bytes=64)
+        nc.gpsimd.memset(w_s_raw[:].bitcast(I32), 0)
+        for q in range(QUADS):
+            nc.sync.dma_start(w_s_raw[32 * q : 32 * q + 4, :].bitcast(I32), wr_scales[0, 4 * q : 4 * q + 4, :].bitcast(I32))
+        for q in range(QUADS):
+            nc.sync.dma_start(w_s_raw[32 * q + 4 : 32 * q + 12, :].bitcast(I32), uc_scales[:, 4 * q : 4 * q + 4, :].bitcast(I32))
+        w_s = keep.tile([P, H], U8, name="w_s", align_bytes=64)
+
+        state = [[keep.tile([P, T], F32, name="state%d_%d" % (a, t)) for t in range(PACK)] for a in range(GROUPS)]
+
+        def load_state(a):
+            rows = gT[GROUP * a : GROUP * (a + 1), :].rearrange("(p t) w -> p t w", t=PACK)
+            for t in range(PACK):
+                nc.sync.dma_start(state[a][t][:], rows[:, t, :])
+
+        wc_codes = [keep.tile([P, GROUP], U32, name="wc_codes%d" % g, align_bytes=64) for g in range(GROUPS)]
+        wc_s = [keep.tile([P, GROUP], U8, name="wc_s%d" % g, align_bytes=64) for g in range(GROUPS)]
+        uc_w = [[keep.tile([P, GROUP], I32, name="uc_w%d_%d" % (a, g), align_bytes=64) for g in range(GROUPS)] for a in range(GROUPS)]
+        wc_raw = [ring.tile([P, PACK, GROUP], F32, name="wc_raw%d" % g, tag="rows", bufs=4) for g in range(GROUPS)]
+        uc_raw = [[keep.tile([P, GROUP], I32, name="uc_raw%d_%d" % (a, g)) for g in range(GROUPS)] for a in range(GROUPS)]
+
+        def load_wc(g):
+            cols = slice(GROUP * g, GROUP * (g + 1))
+            nc.sync.dma_start(wc_raw[g][:], wc[:, cols].rearrange("(p j) n -> p j n", j=PACK))
+
+        def load_uc(g):
+            cols = slice(GROUP * g, GROUP * (g + 1))
+            for a in range(GROUPS):
+                nc.sync.dma_start(uc_raw[a][g][:], uc_words[a, :, cols, :].rearrange("p e i -> p (e i)").bitcast(I32))
+
+        def prepare_weights(g):
+            wc_bf = ring.tile([P, GROUP * PACK], BF16, name="wc_bf", align_bytes=64)
+            nc.scalar.copy(
+                out=wc_bf[:].rearrange("p (t m j) -> p m t j", t=PACK, j=PACK),
+                in_=wc_raw[g][:].rearrange("p j (m t) -> p m t j", t=PACK),
+            )
+            for a in range(GROUPS):
+                nc.vector.tensor_copy(
+                    out=uc_w[a][g][:].rearrange("p (t c i) -> p c t i", t=PACK, i=RUN),
+                    in_=uc_raw[a][g][:].rearrange("p (c i t) -> p c t i", t=PACK, i=RUN),
+                )
+            nc.vector.quantize_mx(out=wc_codes[g][:].bitcast(FP8X4), scales=wc_s[g][:], in_=wc_bf[:])
+
+        bias = keep.tile([P, GROUPS, PACK], F32, name="bias")
+        gains = keep.tile([P, GROUPS, PACK], F32, name="gains")
+
+        load_state(0)
+        load_wc(0)
+        load_wc(1)
+        nc.sync.dma_start(bias[:], b.rearrange("(g p t) -> p g t", p=P, t=PACK))
+        nc.sync.dma_start(gains[:], gain.rearrange("(g p t) -> p g t", p=P, t=PACK))
+        load_state(1)
+        load_uc(0)
+        load_uc(1)
+
+        v_w, v_s = [], []
+        for s, (j0, n) in enumerate(SLICES):
+            picks = offsets[:, j0 // 16 : (j0 + n) // 16]
+            words = keep.tile([P, n], U32, name="v_w%d" % s, align_bytes=64)
+            scales = keep.tile([P, n], U8, name="v_s%d" % s, align_bytes=64)
+            nc.vector.tensor_copy(words[:], tab_w[:].bitcast(U32).indirect(picks))
+            nc.vector.tensor_copy(scales[:], tab_s[:].indirect(picks))
+            v_w.append(words)
+            v_s.append(scales)
+            if s == 0:
+                nc.vector.tensor_copy(
+                    out=w_s[:].rearrange("p (t c i) -> p c t i", t=PACK, i=16),
+                    in_=w_s_raw[:].rearrange("p (c i t) -> p c t i", t=PACK, i=16),
+                )
+
+        def dealt(g, t):
+            return slice(t * (H // PACK) + g * P, t * (H // PACK) + (g + 1) * P)
+
+        gate = {}
+        for s, (j0, n) in enumerate(SLICES):
+            for a in range(GROUPS):
+                gate[a, s] = keep.tile([P, PACK, n], F32, name="gate%d_%d" % (a, s))
+                for t in range(PACK):
+                    acc = psum.tile([P, WIDEST], F32, name="acc")
+                    cols = dealt(a, t)
+                    nc.tensor.matmul_mx(
+                        out=acc[:, :n],
+                        lhsT=wr_w[:, 2 * cols.start : 2 * cols.stop].bitcast(FP4X4),
+                        lhsT_scale=w_s[:, cols],
+                        rhs=v_w[s][:].bitcast(FP8X4),
+                        rhs_scale=v_s[s][:],
+                        start=True,
+                        stop=True,
+                    )
+                    nc.scalar.activation(out=gate[a, s][:, t, :], in_=acc[:, :n], func=ACT.Sigmoid)
+
+        picked = [keep.tile([P, PACK * WIDEST], F32, name="picked%d" % a) for a in range(GROUPS)]
+        first = keep.tile([P, PACK * 256], F32, name="first")
+        room = {
+            (0, 0): first[:],
+            (0, 1): picked[0][:],
+            (1, 0): picked[1][:, 1024:],
+            (1, 1): picked[1][:],
+            (0, 2): gate[1, 0][:].rearrange("p t n -> p (t n)"),
+            (1, 2): picked[1][:, :1024],
+        }
+        h_w, h_s = {}, {}
+
+        def make_h(a, s):
+            j0, n = SLICES[s]
+            picks = offsets[:, j0 // 16 : (j0 + n) // 16]
+            prev = room[a, s]
+            for t in range(PACK):
+                nc.vector.tensor_copy(prev[:, t * n : (t + 1) * n], state[a][t][:].indirect(picks))
+            h_bf = ring.tile([P, PACK * WIDEST], BF16, name="h_bf", align_bytes=64)
+            nc.vector.tensor_tensor(
+                out=h_bf[:, : PACK * n].rearrange("p (c i t) -> p c t i", t=PACK, i=RUN),
+                in0=prev.rearrange("p (t c i) -> p c t i", t=PACK, i=RUN),
+                in1=gate[a, s][:].rearrange("p t (c i) -> p c t i", i=RUN),
+                op=MULT,
+            )
+            h_w[a, s] = keep.tile([P, n], U32, name="h_w%d_%d" % (a, s), align_bytes=64)
+            h_s[a, s] = keep.tile([P, n], U8, name="h_s%d_%d" % (a, s), align_bytes=64)
+            nc.vector.quantize_mx(out=h_w[a, s][:].bitcast(FP8X4), scales=h_s[a, s][:], in_=h_bf[:, : PACK * n])
+
+        y_s = keep.tile([P, S], U8, name="y_s", align_bytes=64)
+
+        def make_y(g, s, gain_on_scalar, on_scalar):
+            j0, n = SLICES[s]
+            y = ring.tile([P, PACK * WIDEST], F32, name="y", tag="rows", bufs=4)
+            for t in range(PACK):
+                acc = psum.tile([P, WIDEST], F32, name="acc")
+                own = slice(t * P, (t + 1) * P)
+                nc.tensor.matmul_mx(
+                    out=acc[:, :n],
+                    lhsT=wc_codes[g][:, own].bitcast(FP8X4),
+                    lhsT_scale=wc_s[g][:, own],
+                    rhs=v_w[s][:].bitcast(FP8X4),
+                    rhs_scale=v_s[s][:],
+                    start=True,
+                    stop=False,
+                )
+                for a in range(GROUPS):
+                    nc.tensor.matmul_mx(
+                        out=acc[:, :n],
+                        lhsT=uc_w[a][g][:, own].bitcast(FP8X4),
+                        lhsT_scale=w_s[4 * (a + 1) :, dealt(g, t)],
+                        rhs=h_w[a, s][:].bitcast(FP8X4),
+                        rhs_scale=h_s[a, s][:],
+                        start=False,
+                        stop=(a == GROUPS - 1),
+                    )
+                row = y[:, t * n : (t + 1) * n]
+                nc.scalar.activation(out=row, in_=acc[:, :n], func=ACT.Tanh, bias=bias[:, g, t : t + 1])
+                if gain_on_scalar:
+                    nc.scalar.activation(out=row, in_=row, func=ACT.Copy, scale=gains[:, g, t : t + 1])
+                else:
+                    nc.vector.tensor_scalar(out=row, in0=row, scalar1=gains[:, g, t : t + 1], scalar2=None, op0=MULT)
+            rows = out_0[GROUP * g : GROUP * (g + 1), j0 : j0 + n].rearrange("(p t) j -> p t j", t=PACK)
+            nc.sync.dma_start(rows, y[:, : PACK * n].rearrange("p (t j) -> p t j", t=PACK))
+            y_bf = ring.tile([P, PACK * WIDEST], BF16, name="y_bf", align_bytes=64)
+            woven = y_bf[:, : PACK * n].rearrange("p (c i t) -> p c t i", t=PACK, i=RUN)
+            planar = y[:, : PACK * n].rearrange("p (t c i) -> p c t i", t=PACK, i=RUN)
+            if on_scalar:
+                nc.scalar.copy(out=woven, in_=planar)
+            else:
+                nc.vector.tensor_copy(out=woven, in_=planar)
+            y_w = keep.tile([P, n], U32, name="y_w%d_%d" % (g, s), align_bytes=64)
+            nc.vector.quantize_mx(out=y_w[:].bitcast(FP8X4), scales=y_s[4 * g :, j0 : j0 + n], in_=y_bf[:, : PACK * n])
+            nc.sync.dma_start(
+                out_1[g, :, j0 : j0 + n, :].rearrange("p m t -> p (m t)").bitcast(I32), y_w[:].bitcast(I32)
+            )
+
+        make_h(0, 0)
+        prepare_weights(0)
+        make_h(1, 0)
+        prepare_weights(1)
+        make_h(0, 1)
+        make_h(1, 1)
+        make_y(0, 0, True, True)
+        make_y(1, 0, True, True)
+        make_h(0, 2)
+        make_h(1, 2)
+        make_y(0, 1, True, True)
+        make_y(1, 1, False, False)
+        make_y(0, 2, False, False)
+        make_y(1, 2, True, False)
+        for q in range(QUADS):
+            nc.sync.dma_start(out_2[:, 4 * q : 4 * q + 4, :].bitcast(I32), y_s[32 * q : 32 * q + 8, :].bitcast(I32))

@@ -35,6 +35,10 @@ def tile_list_gru_token_candidate_kernel(
         ring = ctx.enter_context(tc.tile_pool(name="ring", bufs=2))
         psum = ctx.enter_context(tc.psum_pool(name="psum", bufs=8))
 
+        warm = keep.tile([P, 2], F32, name="warm")
+        nc.vector.memset(warm[:], 0.0)
+        nc.scalar.activation(out=warm[:, 1:2], in_=warm[:, 0:1], func=ACT.Sigmoid)
+
         offsets = keep.tile([P, S // 16], U16, name="offsets")
         nc.sync.dma_start(offsets[:], offs)
 
@@ -42,30 +46,15 @@ def tile_list_gru_token_candidate_kernel(
         nc.sync.dma_start(wr_raw[:].bitcast(I32), wr_words[0].bitcast(I32))
         tab_w = keep.tile([P, T], I32, name="tab_w", align_bytes=64)
         nc.sync.dma_start(tab_w[:], tab_words[0].rearrange("p t i -> p (t i)").bitcast(I32))
-        tab_s = keep.tile([P, T], U8, name="tab_s", align_bytes=64)
-        nc.gpsimd.memset(tab_s[:].bitcast(I32), 0)
+        wr_s_raw = keep.tile([P, H], U8, name="wr_s_raw", align_bytes=64)
+        nc.vector.memset(wr_s_raw[:].bitcast(I32), 0)
         for q in range(QUADS):
-            nc.sync.dma_start(tab_s[32 * q : 32 * q + 4, :].bitcast(I32), tab_scales[0, 4 * q : 4 * q + 4, :].bitcast(I32))
-
-        wr_w = keep.tile([P, 2 * H], U8, name="wr_w", align_bytes=64)
-        nc.vector.tensor_copy(
-            out=wr_w[:].bitcast(U16).rearrange("p (t c i) -> p c t i", t=PACK, i=8),
-            in_=wr_raw[:].bitcast(U16).rearrange("p (c i t) -> p c t i", t=PACK, i=8),
-        )
-        w_s_raw = keep.tile([P, H], U8, name="w_s_raw", align_bytes=64)
-        nc.gpsimd.memset(w_s_raw[:].bitcast(I32), 0)
-        for q in range(QUADS):
-            nc.sync.dma_start(w_s_raw[32 * q : 32 * q + 4, :].bitcast(I32), wr_scales[0, 4 * q : 4 * q + 4, :].bitcast(I32))
-        for q in range(QUADS):
-            nc.sync.dma_start(w_s_raw[32 * q + 4 : 32 * q + 12, :].bitcast(I32), uc_scales[:, 4 * q : 4 * q + 4, :].bitcast(I32))
-        w_s = keep.tile([P, H], U8, name="w_s", align_bytes=64)
-
+            nc.sync.dma_start(wr_s_raw[32 * q : 32 * q + 4, :].bitcast(I32), wr_scales[0, 4 * q : 4 * q + 4, :].bitcast(I32))
         state = [[keep.tile([P, T], F32, name="state%d_%d" % (a, t)) for t in range(PACK)] for a in range(GROUPS)]
 
-        def load_state(a):
+        def load_state(a, t):
             rows = gT[GROUP * a : GROUP * (a + 1), :].rearrange("(p t) w -> p t w", t=PACK)
-            for t in range(PACK):
-                nc.sync.dma_start(state[a][t][:], rows[:, t, :])
+            nc.sync.dma_start(state[a][t][:], rows[:, t, :])
 
         wc_codes = [keep.tile([P, GROUP], U32, name="wc_codes%d" % g, align_bytes=64) for g in range(GROUPS)]
         wc_s = [keep.tile([P, GROUP], U8, name="wc_s%d" % g, align_bytes=64) for g in range(GROUPS)]
@@ -82,95 +71,128 @@ def tile_list_gru_token_candidate_kernel(
             for a in range(GROUPS):
                 nc.sync.dma_start(uc_raw[a][g][:], uc_words[a, :, cols, :].rearrange("p e i -> p (e i)").bitcast(I32))
 
-        def prepare_weights(g):
+        tab_s = keep.tile([P, T], U8, name="tab_s", align_bytes=64)
+        nc.gpsimd.memset(tab_s[:].bitcast(I32), 0)
+        for q in range(QUADS):
+            nc.sync.dma_start(tab_s[32 * q : 32 * q + 4, :].bitcast(I32), tab_scales[0, 4 * q : 4 * q + 4, :].bitcast(I32))
+            if q == 0:
+                load_wc(0)
+
+        wr_w = keep.tile([P, 2 * H], U8, name="wr_w", align_bytes=64)
+        nc.vector.tensor_copy(
+            out=wr_w[:].bitcast(U16).rearrange("p (t c i) -> p c t i", t=PACK, i=8),
+            in_=wr_raw[:].bitcast(U16).rearrange("p (c i t) -> p c t i", t=PACK, i=8),
+        )
+        uc_s_raw = keep.tile([P, H], U8, name="uc_s_raw", align_bytes=64)
+        nc.gpsimd.memset(uc_s_raw[:].bitcast(I32), 0)
+        wr_s = keep.tile([P, H], U8, name="wr_s", align_bytes=64)
+        uc_s = keep.tile([P, H], U8, name="uc_s", align_bytes=64)
+
+        def deal_scales(dealt_s, raw):
+            nc.vector.tensor_copy(
+                out=dealt_s[:].rearrange("p (t c i) -> p c t i", t=PACK, i=16),
+                in_=raw[:].rearrange("p (c i t) -> p c t i", t=PACK, i=16),
+            )
+
+        def quantise_wc(g):
             wc_bf = ring.tile([P, GROUP * PACK], BF16, name="wc_bf", align_bytes=64)
             nc.scalar.copy(
                 out=wc_bf[:].rearrange("p (t m j) -> p m t j", t=PACK, j=PACK),
                 in_=wc_raw[g][:].rearrange("p j (m t) -> p m t j", t=PACK),
             )
+            nc.vector.quantize_mx(out=wc_codes[g][:].bitcast(FP8X4), scales=wc_s[g][:], in_=wc_bf[:])
+
+        def deal_uc(g):
             for a in range(GROUPS):
                 nc.vector.tensor_copy(
                     out=uc_w[a][g][:].rearrange("p (t c i) -> p c t i", t=PACK, i=RUN),
                     in_=uc_raw[a][g][:].rearrange("p (c i t) -> p c t i", t=PACK, i=RUN),
                 )
-            nc.vector.quantize_mx(out=wc_codes[g][:].bitcast(FP8X4), scales=wc_s[g][:], in_=wc_bf[:])
 
         bias = keep.tile([P, GROUPS, PACK], F32, name="bias")
         gains = keep.tile([P, GROUPS, PACK], F32, name="gains")
 
-        load_state(0)
-        load_wc(0)
+        for t in range(PACK):
+            load_state(0, t)
         load_wc(1)
+        for q in range(QUADS):
+            nc.sync.dma_start(uc_s_raw[32 * q : 32 * q + 8, :].bitcast(I32), uc_scales[:, 4 * q : 4 * q + 4, :].bitcast(I32))
+        for t in range(PACK):
+            load_state(1, t)
+        load_uc(0)
         nc.sync.dma_start(bias[:], b.rearrange("(g p t) -> p g t", p=P, t=PACK))
         nc.sync.dma_start(gains[:], gain.rearrange("(g p t) -> p g t", p=P, t=PACK))
-        load_state(1)
-        load_uc(0)
         load_uc(1)
 
-        v_w, v_s = [], []
-        for s, (j0, n) in enumerate(SLICES):
-            picks = offsets[:, j0 // 16 : (j0 + n) // 16]
-            words = keep.tile([P, n], U32, name="v_w%d" % s, align_bytes=64)
-            scales = keep.tile([P, n], U8, name="v_s%d" % s, align_bytes=64)
-            nc.vector.tensor_copy(words[:], tab_w[:].bitcast(U32).indirect(picks))
-            nc.vector.tensor_copy(scales[:], tab_s[:].indirect(picks))
-            v_w.append(words)
-            v_s.append(scales)
-            if s == 0:
-                nc.vector.tensor_copy(
-                    out=w_s[:].rearrange("p (t c i) -> p c t i", t=PACK, i=16),
-                    in_=w_s_raw[:].rearrange("p (c i t) -> p c t i", t=PACK, i=16),
-                )
+        v_w = keep.tile([P, S], U32, name="v_w", align_bytes=64)
+        v_s = keep.tile([P, S], U8, name="v_s", align_bytes=64)
+
+        def picks(j0, n):
+            return offsets[:, j0 // 16 : (j0 + n) // 16]
+
+        for j0 in range(0, S, WIDEST):
+            nc.vector.tensor_copy(v_w[:, j0 : j0 + WIDEST], tab_w[:].bitcast(U32).indirect(picks(j0, WIDEST)))
+            if j0 == 0:
+                deal_scales(wr_s, wr_s_raw)
+            nc.vector.tensor_copy(v_s[:, j0 : j0 + WIDEST], tab_s[:].indirect(picks(j0, WIDEST)))
 
         def dealt(g, t):
             return slice(t * (H // PACK) + g * P, t * (H // PACK) + (g + 1) * P)
 
-        gate = {}
-        for s, (j0, n) in enumerate(SLICES):
-            for a in range(GROUPS):
-                gate[a, s] = keep.tile([P, PACK, n], F32, name="gate%d_%d" % (a, s))
-                for t in range(PACK):
-                    acc = psum.tile([P, WIDEST], F32, name="acc")
-                    cols = dealt(a, t)
-                    nc.tensor.matmul_mx(
-                        out=acc[:, :n],
-                        lhsT=wr_w[:, 2 * cols.start : 2 * cols.stop].bitcast(FP4X4),
-                        lhsT_scale=w_s[:, cols],
-                        rhs=v_w[s][:].bitcast(FP8X4),
-                        rhs_scale=v_s[s][:],
-                        start=True,
-                        stop=True,
-                    )
-                    nc.scalar.activation(out=gate[a, s][:, t, :], in_=acc[:, :n], func=ACT.Sigmoid)
+        gate = [keep.tile([P, PACK * S], F32, name="gate%d" % a, align_bytes=64) for a in range(GROUPS)]
 
-        picked = [keep.tile([P, PACK * WIDEST], F32, name="picked%d" % a) for a in range(GROUPS)]
-        first = keep.tile([P, PACK * 256], F32, name="first")
-        room = {
-            (0, 0): first[:],
-            (0, 1): picked[0][:],
-            (1, 0): picked[1][:, 1024:],
-            (1, 1): picked[1][:],
-            (0, 2): gate[1, 0][:].rearrange("p t n -> p (t n)"),
-            (1, 2): picked[1][:, :1024],
-        }
-        h_w, h_s = {}, {}
-
-        def make_h(a, s):
-            j0, n = SLICES[s]
-            picks = offsets[:, j0 // 16 : (j0 + n) // 16]
-            prev = room[a, s]
+        def make_gates(a, j0):
             for t in range(PACK):
-                nc.vector.tensor_copy(prev[:, t * n : (t + 1) * n], state[a][t][:].indirect(picks))
+                acc = psum.tile([P, WIDEST], F32, name="acc")
+                cols = dealt(a, t)
+                nc.tensor.matmul_mx(
+                    out=acc[:],
+                    lhsT=wr_w[:, 2 * cols.start : 2 * cols.stop].bitcast(FP4X4),
+                    lhsT_scale=wr_s[:, cols],
+                    rhs=v_w[:, j0 : j0 + WIDEST].bitcast(FP8X4),
+                    rhs_scale=v_s[:, j0 : j0 + WIDEST],
+                    start=True,
+                    stop=True,
+                )
+                nc.scalar.activation(out=gate[a][:, t * S + j0 : t * S + j0 + WIDEST], in_=acc[:], func=ACT.Sigmoid)
+
+        early = keep.tile([P, PACK * WIDEST], F32, name="early")
+        h_w = [keep.tile([P, S], U32, name="h_w%d" % a, align_bytes=64) for a in range(GROUPS)]
+        h_s = [keep.tile([P, S], U8, name="h_s%d" % a, align_bytes=64) for a in range(GROUPS)]
+
+        def gated_state(a, j0, n, room, at):
+            width = room.shape[1] // PACK
+            for t in range(PACK):
+                nc.vector.tensor_tensor(
+                    room[:, t * width + at : t * width + at + n],
+                    state[a][t][:].indirect(picks(j0, n)),
+                    gate[a][:, t * S + j0 : t * S + j0 + n],
+                    MULT,
+                )
+            return room[:].rearrange("p (t w) -> p t w", t=PACK)[:, :, at : at + n]
+
+        def quantise_h(a, j0, n, h_bf):
+            nc.vector.quantize_mx(out=h_w[a][:, j0 : j0 + n].bitcast(FP8X4), scales=h_s[a][:, j0 : j0 + n], in_=h_bf)
+
+        def make_h(a, j0, n, room, at, weave):
+            planar = gated_state(a, j0, n, room, at)
             h_bf = ring.tile([P, PACK * WIDEST], BF16, name="h_bf", align_bytes=64)
-            nc.vector.tensor_tensor(
+            weave(
                 out=h_bf[:, : PACK * n].rearrange("p (c i t) -> p c t i", t=PACK, i=RUN),
-                in0=prev.rearrange("p (t c i) -> p c t i", t=PACK, i=RUN),
-                in1=gate[a, s][:].rearrange("p t (c i) -> p c t i", i=RUN),
-                op=MULT,
+                in_=planar.rearrange("p t (c i) -> p c t i", i=RUN),
             )
-            h_w[a, s] = keep.tile([P, n], U32, name="h_w%d_%d" % (a, s), align_bytes=64)
-            h_s[a, s] = keep.tile([P, n], U8, name="h_s%d_%d" % (a, s), align_bytes=64)
-            nc.vector.quantize_mx(out=h_w[a, s][:].bitcast(FP8X4), scales=h_s[a, s][:], in_=h_bf[:, : PACK * n])
+            quantise_h(a, j0, n, h_bf[:, : PACK * n])
+
+        def make_h_in_place(a, j0, n, room, at):
+            planar = gated_state(a, j0, n, room, at)
+            part = n // PACK
+            rows_bf = room[:].bitcast(BF16).rearrange("p (r w) -> p r w", r=PACK)[:, :, 2 * (at + n) : 2 * (at + n) + n]
+            nc.vector.tensor_copy(
+                out=rows_bf.rearrange("p r (c i t) -> p r c t i", t=PACK, i=RUN),
+                in_=planar.rearrange("p t (r c i) -> p r c t i", r=PACK, i=RUN),
+            )
+            for r in range(PACK):
+                quantise_h(a, j0 + r * part, part, rows_bf[:, r, :])
 
         y_s = keep.tile([P, S], U8, name="y_s", align_bytes=64)
 
@@ -184,8 +206,8 @@ def tile_list_gru_token_candidate_kernel(
                     out=acc[:, :n],
                     lhsT=wc_codes[g][:, own].bitcast(FP8X4),
                     lhsT_scale=wc_s[g][:, own],
-                    rhs=v_w[s][:].bitcast(FP8X4),
-                    rhs_scale=v_s[s][:],
+                    rhs=v_w[:, j0 : j0 + n].bitcast(FP8X4),
+                    rhs_scale=v_s[:, j0 : j0 + n],
                     start=True,
                     stop=False,
                 )
@@ -193,9 +215,9 @@ def tile_list_gru_token_candidate_kernel(
                     nc.tensor.matmul_mx(
                         out=acc[:, :n],
                         lhsT=uc_w[a][g][:, own].bitcast(FP8X4),
-                        lhsT_scale=w_s[4 * (a + 1) :, dealt(g, t)],
-                        rhs=h_w[a, s][:].bitcast(FP8X4),
-                        rhs_scale=h_s[a, s][:],
+                        lhsT_scale=uc_s[4 * a :, dealt(g, t)],
+                        rhs=h_w[a][:, j0 : j0 + n].bitcast(FP8X4),
+                        rhs_scale=h_s[a][:, j0 : j0 + n],
                         start=False,
                         stop=(a == GROUPS - 1),
                     )
@@ -220,19 +242,25 @@ def tile_list_gru_token_candidate_kernel(
                 out_1[g, :, j0 : j0 + n, :].rearrange("p m t -> p (m t)").bitcast(I32), y_w[:].bitcast(I32)
             )
 
-        make_h(0, 0)
-        prepare_weights(0)
-        make_h(1, 0)
-        prepare_weights(1)
-        make_h(0, 1)
-        make_h(1, 1)
+        make_gates(0, 0)
+        make_gates(0, 512)
+        make_gates(1, 0)
+        make_h(0, 0, 512, early, 0, nc.scalar.copy)
+        quantise_wc(0)
+        deal_scales(uc_s, uc_s_raw)
+        make_h(0, 512, 512, gate[1], 512, nc.scalar.copy)
+        quantise_wc(1)
+        make_gates(1, 512)
+        make_h_in_place(1, 0, 256, gate[0], 0)
+        deal_uc(0)
+        deal_uc(1)
+        make_h_in_place(1, 256, 512, gate[0], 256)
         make_y(0, 0, True, True)
         make_y(1, 0, True, True)
-        make_h(0, 2)
-        make_h(1, 2)
-        make_y(0, 1, True, True)
+        make_h(1, 768, 256, gate[0], 768, nc.vector.tensor_copy)
+        make_y(0, 1, False, False)
         make_y(1, 1, False, False)
-        make_y(0, 2, False, False)
+        make_y(0, 2, True, False)
         make_y(1, 2, True, False)
         for q in range(QUADS):
             nc.sync.dma_start(out_2[:, 4 * q : 4 * q + 4, :].bitcast(I32), y_s[32 * q : 32 * q + 8, :].bitcast(I32))

@@ -94,13 +94,12 @@ def tile_list_gru_token_candidate_kernel(
                 in_=raw[:].rearrange("p (c i t) -> p c t i", t=PACK, i=16),
             )
 
-        def quantise_wc(g):
-            wc_bf = ring.tile([P, GROUP * PACK], BF16, name="wc_bf", align_bytes=64)
+        def quantise_wc(g, wc_bf):
             nc.scalar.copy(
-                out=wc_bf[:].rearrange("p (t m j) -> p m t j", t=PACK, j=PACK),
+                out=wc_bf.rearrange("p (t m j) -> p m t j", t=PACK, j=PACK),
                 in_=wc_raw[g][:].rearrange("p j (m t) -> p m t j", t=PACK),
             )
-            nc.vector.quantize_mx(out=wc_codes[g][:].bitcast(FP8X4), scales=wc_s[g][:], in_=wc_bf[:])
+            nc.vector.quantize_mx(out=wc_codes[g][:].bitcast(FP8X4), scales=wc_s[g][:], in_=wc_bf)
 
         def deal_uc(g):
             for a in range(GROUPS):
@@ -114,7 +113,6 @@ def tile_list_gru_token_candidate_kernel(
 
         for t in range(PACK):
             load_state(0, t)
-        load_wc(1)
         for q in range(QUADS):
             nc.sync.dma_start(uc_s_raw[32 * q : 32 * q + 8, :].bitcast(I32), uc_scales[:, 4 * q : 4 * q + 4, :].bitcast(I32))
         for t in range(PACK):
@@ -122,6 +120,7 @@ def tile_list_gru_token_candidate_kernel(
         load_uc(0)
         nc.sync.dma_start(bias[:], b.rearrange("(g p t) -> p g t", p=P, t=PACK))
         nc.sync.dma_start(gains[:], gain.rearrange("(g p t) -> p g t", p=P, t=PACK))
+        load_wc(1)
         load_uc(1)
 
         v_w = keep.tile([P, S], U32, name="v_w", align_bytes=64)
@@ -141,8 +140,8 @@ def tile_list_gru_token_candidate_kernel(
 
         gate = [keep.tile([P, PACK * S], F32, name="gate%d" % a, align_bytes=64) for a in range(GROUPS)]
 
-        def make_gates(a, j0):
-            for t in range(PACK):
+        def make_gates(a, j0, planes=range(PACK)):
+            for t in planes:
                 acc = psum.tile([P, WIDEST], F32, name="acc")
                 cols = dealt(a, t)
                 nc.tensor.matmul_mx(
@@ -242,17 +241,19 @@ def tile_list_gru_token_candidate_kernel(
                 out_1[g, :, j0 : j0 + n, :].rearrange("p m t -> p (m t)").bitcast(I32), y_w[:].bitcast(I32)
             )
 
-        make_gates(0, 0)
-        make_gates(0, 512)
+        for t in range(PACK):
+            make_gates(0, 0, [t])
+            make_gates(0, 512, [t])
         make_gates(1, 0)
         make_h(0, 0, 512, early, 0, nc.scalar.copy)
-        quantise_wc(0)
+        wc_first = keep.tile([P, GROUP * PACK], BF16, name="wc_first", align_bytes=64)
+        quantise_wc(0, wc_first[:])
         deal_scales(uc_s, uc_s_raw)
         make_h(0, 512, 512, gate[1], 512, nc.scalar.copy)
-        quantise_wc(1)
         make_gates(1, 512)
         make_h_in_place(1, 0, 256, gate[0], 0)
         deal_uc(0)
+        quantise_wc(1, gate[0][:, (PACK - 1) * S :].bitcast(BF16))
         deal_uc(1)
         make_h_in_place(1, 256, 512, gate[0], 256)
         make_y(0, 0, True, True)

@@ -22,8 +22,7 @@ GROUP = P * PACK
 GROUPS = H // GROUP
 QUADS = 4
 RUN = 4
-SLICES = ((0, 256), (256, 512), (768, 256))
-WIDEST = 512
+BANK = 512
 
 
 def tile_list_gru_token_candidate_kernel(
@@ -35,233 +34,265 @@ def tile_list_gru_token_candidate_kernel(
         ring = ctx.enter_context(tc.tile_pool(name="ring", bufs=2))
         psum = ctx.enter_context(tc.psum_pool(name="psum", bufs=8))
 
-        warm = keep.tile([P, 2], F32, name="warm")
-        nc.vector.memset(warm[:], 0.0)
-        nc.scalar.activation(out=warm[:, 1:2], in_=warm[:, 0:1], func=ACT.Sigmoid)
+        def rows_tile(name, shape):
+            return ring.tile(shape, F32, name=name, tag="rows", bufs=10)
 
         offsets = keep.tile([P, S // 16], U16, name="offsets")
-        nc.sync.dma_start(offsets[:], offs)
-
-        wr_raw = keep.tile([P, 2 * H], U8, name="wr_raw", align_bytes=64)
-        nc.sync.dma_start(wr_raw[:].bitcast(I32), wr_words[0].bitcast(I32))
+        tab_s = keep.tile([P, T], U8, name="tab_s", align_bytes=64)
         tab_w = keep.tile([P, T], I32, name="tab_w", align_bytes=64)
-        nc.sync.dma_start(tab_w[:], tab_words[0].rearrange("p t i -> p (t i)").bitcast(I32))
-        wr_s_raw = keep.tile([P, H], U8, name="wr_s_raw", align_bytes=64)
-        nc.vector.memset(wr_s_raw[:].bitcast(I32), 0)
-        for q in range(QUADS):
-            nc.sync.dma_start(wr_s_raw[32 * q : 32 * q + 4, :].bitcast(I32), wr_scales[0, 4 * q : 4 * q + 4, :].bitcast(I32))
-        state = [[keep.tile([P, T], F32, name="state%d_%d" % (a, t)) for t in range(PACK)] for a in range(GROUPS)]
-
-        def load_state(a, t):
-            rows = gT[GROUP * a : GROUP * (a + 1), :].rearrange("(p t) w -> p t w", t=PACK)
-            nc.sync.dma_start(state[a][t][:], rows[:, t, :])
-
+        wr_raw = keep.tile([P, 2 * H], U8, name="wr_raw", align_bytes=64)
+        wr_w = keep.tile([P, 2 * H], U8, name="wr_w", align_bytes=64)
+        wr_s_raw = keep.tile([P, H], U8, name="wr_s_raw", tag="late_words", align_bytes=64)
+        uc_s_raw = keep.tile([P, H], U8, name="uc_s_raw", align_bytes=64)
+        wr_s = keep.tile([P, H], U8, name="wr_s", align_bytes=64)
+        uc_s = keep.tile([P, H], U8, name="uc_s", align_bytes=64)
         wc_codes = [keep.tile([P, GROUP], U32, name="wc_codes%d" % g, align_bytes=64) for g in range(GROUPS)]
         wc_s = [keep.tile([P, GROUP], U8, name="wc_s%d" % g, align_bytes=64) for g in range(GROUPS)]
         uc_w = [[keep.tile([P, GROUP], I32, name="uc_w%d_%d" % (a, g), align_bytes=64) for g in range(GROUPS)] for a in range(GROUPS)]
-        wc_raw = [ring.tile([P, PACK, GROUP], F32, name="wc_raw%d" % g, tag="rows", bufs=4) for g in range(GROUPS)]
         uc_raw = [[keep.tile([P, GROUP], I32, name="uc_raw%d_%d" % (a, g)) for g in range(GROUPS)] for a in range(GROUPS)]
+        bias = keep.tile([P, GROUPS, PACK], F32, name="bias", tag="after_tanh", align_bytes=64)
+        gains = keep.tile([P, GROUPS, PACK], F32, name="gains")
+        v_w = {}
+        v_s = keep.tile([P, S], U8, name="v_s", align_bytes=64)
+        gate_pairs = [keep.tile([P, 2, S], F32, name="gate0_%d" % u, tag="room%d" % u, align_bytes=64) for u in range(2)]
+        gate = {(0, t): gate_pairs[t // 2][:, t % 2, :] for t in range(PACK)}
+        for t in range(PACK):
+            gate[1, t] = keep.tile([P, S], F32, name="gate1_%d" % t)[:]
+        early = keep.tile([P, PACK * S], F32, name="early")
+        h_w = [keep.tile([P, S], U32, name="h_w%d" % a, align_bytes=64) for a in range(GROUPS)]
+        h_s = [keep.tile([P, S], U8, name="h_s%d" % a, align_bytes=64) for a in range(GROUPS)]
+        y_s = keep.tile([P, S], U8, name="y_s", align_bytes=64)
+        state = {}
+        wc_raw = {}
+
+        def load_scale_rows(plane, rows, count):
+            for q in range(QUADS):
+                nc.sync.dma_start(plane[32 * q : 32 * q + count, :].bitcast(I32), rows[:, 4 * q : 4 * q + 4, :].bitcast(I32))
+
+        def load_state(a, t):
+            state[a, t] = rows_tile("state%d_%d" % (a, t), [P, T])
+            rows = gT[GROUP * a : GROUP * (a + 1), :].rearrange("(p t) w -> p t w", t=PACK)
+            nc.sync.dma_start(state[a, t][:], rows[:, t, :])
 
         def load_wc(g):
+            wc_raw[g] = rows_tile("wc_raw%d" % g, [P, PACK, GROUP])
+            nc.sync.dma_start(wc_raw[g][:], wc[:, GROUP * g : GROUP * (g + 1)].rearrange("(p j) n -> p j n", j=PACK))
+
+        def load_uc(a, g):
             cols = slice(GROUP * g, GROUP * (g + 1))
-            nc.sync.dma_start(wc_raw[g][:], wc[:, cols].rearrange("(p j) n -> p j n", j=PACK))
+            nc.sync.dma_start(uc_raw[a][g][:], uc_words[a, :, cols, :].rearrange("p e i -> p (e i)").bitcast(I32))
 
-        def load_uc(g):
-            cols = slice(GROUP * g, GROUP * (g + 1))
-            for a in range(GROUPS):
-                nc.sync.dma_start(uc_raw[a][g][:], uc_words[a, :, cols, :].rearrange("p e i -> p (e i)").bitcast(I32))
-
-        tab_s = keep.tile([P, T], U8, name="tab_s", align_bytes=64)
-        nc.gpsimd.memset(tab_s[:].bitcast(I32), 0)
-        for q in range(QUADS):
-            nc.sync.dma_start(tab_s[32 * q : 32 * q + 4, :].bitcast(I32), tab_scales[0, 4 * q : 4 * q + 4, :].bitcast(I32))
-            if q == 0:
-                load_wc(0)
-
-        wr_w = keep.tile([P, 2 * H], U8, name="wr_w", align_bytes=64)
-        nc.vector.tensor_copy(
-            out=wr_w[:].bitcast(U16).rearrange("p (t c i) -> p c t i", t=PACK, i=8),
-            in_=wr_raw[:].bitcast(U16).rearrange("p (c i t) -> p c t i", t=PACK, i=8),
-        )
-        uc_s_raw = keep.tile([P, H], U8, name="uc_s_raw", align_bytes=64)
-        nc.gpsimd.memset(uc_s_raw[:].bitcast(I32), 0)
-        wr_s = keep.tile([P, H], U8, name="wr_s", align_bytes=64)
-        uc_s = keep.tile([P, H], U8, name="uc_s", align_bytes=64)
-
-        def deal_scales(dealt_s, raw):
+        def deal(dst, src, run):
             nc.vector.tensor_copy(
-                out=dealt_s[:].rearrange("p (t c i) -> p c t i", t=PACK, i=16),
-                in_=raw[:].rearrange("p (c i t) -> p c t i", t=PACK, i=16),
+                out=dst.rearrange("p (t c i) -> p c t i", t=PACK, i=run),
+                in_=src.rearrange("p (c i t) -> p c t i", t=PACK, i=run),
             )
-
-        def quantise_wc(g, wc_bf):
-            nc.scalar.copy(
-                out=wc_bf.rearrange("p (t m j) -> p m t j", t=PACK, j=PACK),
-                in_=wc_raw[g][:].rearrange("p j (m t) -> p m t j", t=PACK),
-            )
-            nc.vector.quantize_mx(out=wc_codes[g][:].bitcast(FP8X4), scales=wc_s[g][:], in_=wc_bf)
-
-        def deal_uc(g):
-            for a in range(GROUPS):
-                nc.vector.tensor_copy(
-                    out=uc_w[a][g][:].rearrange("p (t c i) -> p c t i", t=PACK, i=RUN),
-                    in_=uc_raw[a][g][:].rearrange("p (c i t) -> p c t i", t=PACK, i=RUN),
-                )
-
-        bias = keep.tile([P, GROUPS, PACK], F32, name="bias")
-        gains = keep.tile([P, GROUPS, PACK], F32, name="gains")
-
-        for t in range(PACK):
-            load_state(0, t)
-        for q in range(QUADS):
-            nc.sync.dma_start(uc_s_raw[32 * q : 32 * q + 8, :].bitcast(I32), uc_scales[:, 4 * q : 4 * q + 4, :].bitcast(I32))
-        for t in range(PACK):
-            load_state(1, t)
-        load_uc(0)
-        nc.sync.dma_start(bias[:], b.rearrange("(g p t) -> p g t", p=P, t=PACK))
-        nc.sync.dma_start(gains[:], gain.rearrange("(g p t) -> p g t", p=P, t=PACK))
-        load_wc(1)
-        load_uc(1)
-
-        v_w = keep.tile([P, S], U32, name="v_w", align_bytes=64)
-        v_s = keep.tile([P, S], U8, name="v_s", align_bytes=64)
 
         def picks(j0, n):
             return offsets[:, j0 // 16 : (j0 + n) // 16]
 
-        for j0 in range(0, S, WIDEST):
-            nc.vector.tensor_copy(v_w[:, j0 : j0 + WIDEST], tab_w[:].bitcast(U32).indirect(picks(j0, WIDEST)))
-            if j0 == 0:
-                deal_scales(wr_s, wr_s_raw)
-            nc.vector.tensor_copy(v_s[:, j0 : j0 + WIDEST], tab_s[:].indirect(picks(j0, WIDEST)))
-
         def dealt(g, t):
             return slice(t * (H // PACK) + g * P, t * (H // PACK) + (g + 1) * P)
 
-        gate = [keep.tile([P, PACK * S], F32, name="gate%d" % a, align_bytes=64) for a in range(GROUPS)]
+        def make_gate(a, t, j0):
+            acc = psum.tile([P, BANK], F32, name="acc")
+            cols = dealt(a, t)
+            nc.tensor.matmul_mx(
+                out=acc[:],
+                lhsT=wr_w[:, 2 * cols.start : 2 * cols.stop].bitcast(FP4X4),
+                lhsT_scale=wr_s[:, cols],
+                rhs=v_w[j0 // BANK][:].bitcast(FP8X4),
+                rhs_scale=v_s[:, j0 : j0 + BANK],
+                start=True,
+                stop=True,
+            )
+            nc.scalar.activation(out=gate[a, t][:, j0 : j0 + BANK], in_=acc[:], func=ACT.Sigmoid)
 
-        def make_gates(a, j0, planes=range(PACK)):
-            for t in planes:
-                acc = psum.tile([P, WIDEST], F32, name="acc")
-                cols = dealt(a, t)
-                nc.tensor.matmul_mx(
-                    out=acc[:],
-                    lhsT=wr_w[:, 2 * cols.start : 2 * cols.stop].bitcast(FP4X4),
-                    lhsT_scale=wr_s[:, cols],
-                    rhs=v_w[:, j0 : j0 + WIDEST].bitcast(FP8X4),
-                    rhs_scale=v_s[:, j0 : j0 + WIDEST],
-                    start=True,
-                    stop=True,
-                )
-                nc.scalar.activation(out=gate[a][:, t * S + j0 : t * S + j0 + WIDEST], in_=acc[:], func=ACT.Sigmoid)
+        room = {}
 
-        early = keep.tile([P, PACK * WIDEST], F32, name="early")
-        h_w = [keep.tile([P, S], U32, name="h_w%d" % a, align_bytes=64) for a in range(GROUPS)]
-        h_s = [keep.tile([P, S], U8, name="h_s%d" % a, align_bytes=64) for a in range(GROUPS)]
+        def gated(a, j0, n):
+            first = FIRST if (a, j0 >= FIRST) == (1, True) else 0
+            rows = room[a, first][:].rearrange("p (t w) -> p t w", t=PACK)
+            return rows[:, :, j0 - first : j0 - first + n]
 
-        def gated_state(a, j0, n, room, at):
-            width = room.shape[1] // PACK
-            for t in range(PACK):
-                nc.vector.tensor_tensor(
-                    room[:, t * width + at : t * width + at + n],
-                    state[a][t][:].indirect(picks(j0, n)),
-                    gate[a][:, t * S + j0 : t * S + j0 + n],
-                    MULT,
-                )
-            return room[:].rearrange("p (t w) -> p t w", t=PACK)[:, :, at : at + n]
+        def gather_state(a, t, j0, n):
+            nc.vector.tensor_tensor(
+                gated(a, j0, n)[:, t, :],
+                state[a, t][:].indirect(picks(j0, n)),
+                gate[a, t][:, j0 : j0 + n],
+                MULT,
+            )
 
-        def quantise_h(a, j0, n, h_bf):
-            nc.vector.quantize_mx(out=h_w[a][:, j0 : j0 + n].bitcast(FP8X4), scales=h_s[a][:, j0 : j0 + n], in_=h_bf)
-
-        def make_h(a, j0, n, room, at, weave):
-            planar = gated_state(a, j0, n, room, at)
-            h_bf = ring.tile([P, PACK * WIDEST], BF16, name="h_bf", align_bytes=64)
-            weave(
-                out=h_bf[:, : PACK * n].rearrange("p (c i t) -> p c t i", t=PACK, i=RUN),
+        def weave(copy, woven, planar):
+            copy(
+                out=woven.rearrange("p (c i t) -> p c t i", t=PACK, i=RUN),
                 in_=planar.rearrange("p t (c i) -> p c t i", i=RUN),
             )
-            quantise_h(a, j0, n, h_bf[:, : PACK * n])
 
-        def make_h_in_place(a, j0, n, room, at):
-            planar = gated_state(a, j0, n, room, at)
-            part = n // PACK
-            rows_bf = room[:].bitcast(BF16).rearrange("p (r w) -> p r w", r=PACK)[:, :, 2 * (at + n) : 2 * (at + n) + n]
-            nc.vector.tensor_copy(
-                out=rows_bf.rearrange("p r (c i t) -> p r c t i", t=PACK, i=RUN),
-                in_=planar.rearrange("p t (r c i) -> p r c t i", r=PACK, i=RUN),
+        def make_h(a, j0, n, copy, h_bf=None):
+            if h_bf is None:
+                h_bf = ring.tile([P, PACK * BANK], BF16, name="h_bf", align_bytes=64, bufs=3)
+            weave(copy, h_bf[:, : PACK * n], gated(a, j0, n))
+            nc.vector.quantize_mx(
+                out=h_w[a][:, j0 : j0 + n].bitcast(FP8X4), scales=h_s[a][:, j0 : j0 + n], in_=h_bf[:, : PACK * n]
             )
-            for r in range(PACK):
-                quantise_h(a, j0 + r * part, part, rows_bf[:, r, :])
 
-        y_s = keep.tile([P, S], U8, name="y_s", align_bytes=64)
+        def quantise_wc(g, copy, tag):
+            wc_bf = keep.tile([P, PACK * GROUP], BF16, name="wc_bf%d" % g, tag=tag, align_bytes=64)
+            copy(
+                out=wc_bf[:].rearrange("p (t m j) -> p m t j", t=PACK, j=PACK),
+                in_=wc_raw[g][:].rearrange("p j (m t) -> p m t j", t=PACK),
+            )
+            nc.vector.quantize_mx(out=wc_codes[g][:].bitcast(FP8X4), scales=wc_s[g][:], in_=wc_bf[:])
 
-        def make_y(g, s, gain_on_scalar, on_scalar):
-            j0, n = SLICES[s]
-            y = ring.tile([P, PACK * WIDEST], F32, name="y", tag="rows", bufs=4)
-            for t in range(PACK):
-                acc = psum.tile([P, WIDEST], F32, name="acc")
+        y_rows = {}
+
+        sums = {}
+
+        def add_pass(g, j0, n, k, planes=range(PACK)):
+            at = j0 % BANK
+            for t in planes:
+                if k == 0:
+                    sums[g, j0, t] = psum.tile([P, BANK], F32, name="acc")
                 own = slice(t * P, (t + 1) * P)
+                w, w_scale, x, x_scale = [
+                    (uc_w[0][g][:, own], uc_s[:, dealt(g, t)], h_w[0][:, j0 : j0 + n], h_s[0][:, j0 : j0 + n]),
+                    (wc_codes[g][:, own], wc_s[g][:, own], v_w[j0 // BANK][:, at : at + n], v_s[:, j0 : j0 + n]),
+                    (uc_w[1][g][:, own], uc_s[4:, dealt(g, t)], h_w[1][:, j0 : j0 + n], h_s[1][:, j0 : j0 + n]),
+                ][k]
                 nc.tensor.matmul_mx(
-                    out=acc[:, :n],
-                    lhsT=wc_codes[g][:, own].bitcast(FP8X4),
-                    lhsT_scale=wc_s[g][:, own],
-                    rhs=v_w[:, j0 : j0 + n].bitcast(FP8X4),
-                    rhs_scale=v_s[:, j0 : j0 + n],
-                    start=True,
-                    stop=False,
+                    out=sums[g, j0, t][:, :n],
+                    lhsT=w.bitcast(FP8X4),
+                    lhsT_scale=w_scale,
+                    rhs=x.bitcast(FP8X4),
+                    rhs_scale=x_scale,
+                    start=(k == 0),
+                    stop=(k == 2),
                 )
-                for a in range(GROUPS):
-                    nc.tensor.matmul_mx(
-                        out=acc[:, :n],
-                        lhsT=uc_w[a][g][:, own].bitcast(FP8X4),
-                        lhsT_scale=uc_s[4 * a :, dealt(g, t)],
-                        rhs=h_w[a][:, j0 : j0 + n].bitcast(FP8X4),
-                        rhs_scale=h_s[a][:, j0 : j0 + n],
-                        start=False,
-                        stop=(a == GROUPS - 1),
-                    )
-                row = y[:, t * n : (t + 1) * n]
-                nc.scalar.activation(out=row, in_=acc[:, :n], func=ACT.Tanh, bias=bias[:, g, t : t + 1])
-                if gain_on_scalar:
+
+        def make_y(g, j0, n, scalar_gains, stores):
+            if j0 % BANK == 0:
+                y_rows[g, j0 // BANK] = rows_tile("y%d_%d" % (g, j0), [P, PACK * BANK])
+            y = y_rows[g, j0 // BANK][:].rearrange("p (t j) -> p t j", t=PACK)[:, :, j0 % BANK : j0 % BANK + n]
+            rows = out_0[GROUP * g : GROUP * (g + 1), j0 : j0 + n].rearrange("(p t) j -> p t j", t=PACK)
+            for t in range(PACK):
+                for k in range(2 if (g, j0, t) in sums else 0, 3):
+                    add_pass(g, j0, n, k, [t])
+                row = y[:, t, :]
+                nc.scalar.activation(out=row, in_=sums[g, j0, t][:, :n], func=ACT.Tanh, bias=bias[:, g, t : t + 1])
+                if t < scalar_gains:
                     nc.scalar.activation(out=row, in_=row, func=ACT.Copy, scale=gains[:, g, t : t + 1])
                 else:
                     nc.vector.tensor_scalar(out=row, in0=row, scalar1=gains[:, g, t : t + 1], scalar2=None, op0=MULT)
-            rows = out_0[GROUP * g : GROUP * (g + 1), j0 : j0 + n].rearrange("(p t) j -> p t j", t=PACK)
-            nc.sync.dma_start(rows, y[:, : PACK * n].rearrange("p (t j) -> p t j", t=PACK))
-            y_bf = ring.tile([P, PACK * WIDEST], BF16, name="y_bf", align_bytes=64)
-            woven = y_bf[:, : PACK * n].rearrange("p (c i t) -> p c t i", t=PACK, i=RUN)
-            planar = y[:, : PACK * n].rearrange("p (t c i) -> p c t i", t=PACK, i=RUN)
-            if on_scalar:
-                nc.scalar.copy(out=woven, in_=planar)
-            else:
-                nc.vector.tensor_copy(out=woven, in_=planar)
-            y_w = keep.tile([P, n], U32, name="y_w%d_%d" % (g, s), align_bytes=64)
+                each = PACK // stores
+                if (t + 1) % each == 0:
+                    nc.sync.dma_start(rows[:, t + 1 - each : t + 1, :], y[:, t + 1 - each : t + 1, :])
+
+        def open_sums(g, j0, n):
+            add_pass(g, j0, n, 0)
+            add_pass(g, j0, n, 1)
+
+        def make_planes(g, j0, n, copy, y_bf=None):
+            planar = y_rows[g, j0 // BANK][:].rearrange("p (t j) -> p t j", t=PACK)[:, :, j0 % BANK : j0 % BANK + n]
+            if y_bf is None:
+                y_bf = ring.tile([P, PACK * BANK], BF16, name="y_bf", align_bytes=64, bufs=3)
+            weave(copy, y_bf[:, : PACK * n], planar)
+            y_w = keep.tile([P, n], U32, name="y_w%d_%d" % (g, j0), align_bytes=64)
             nc.vector.quantize_mx(out=y_w[:].bitcast(FP8X4), scales=y_s[4 * g :, j0 : j0 + n], in_=y_bf[:, : PACK * n])
             nc.sync.dma_start(
                 out_1[g, :, j0 : j0 + n, :].rearrange("p m t -> p (m t)").bitcast(I32), y_w[:].bitcast(I32)
             )
 
+        on_scalar = nc.scalar.copy
+        on_vector = nc.vector.tensor_copy
+
+
+        nc.gpsimd.memset(tab_s[:].bitcast(I32), 0)
+        nc.vector.memset(wr_s_raw[:].bitcast(I32), 0)
+        nc.gpsimd.memset(uc_s_raw[:].bitcast(I32), 0)
+        warm = keep.tile([P, 2], F32, name="warm")
+        nc.vector.memset(warm[:], 0.0)
+        nc.scalar.activation(out=warm[:, 1:2], in_=warm[:, 0:1], func=ACT.Sigmoid)
+
+        nc.sync.dma_start(offsets[:], offs)
+        load_scale_rows(tab_s, tab_scales, 4)
+        nc.sync.dma_start(wr_raw[:].bitcast(I32), wr_words[0].bitcast(I32))
+        nc.sync.dma_start(tab_w[:], tab_words[0].rearrange("p t i -> p (t i)").bitcast(I32))
+        load_scale_rows(wr_s_raw, wr_scales, 4)
         for t in range(PACK):
-            make_gates(0, 0, [t])
-            make_gates(0, 512, [t])
-        make_gates(1, 0)
-        make_h(0, 0, 512, early, 0, nc.scalar.copy)
-        wc_first = keep.tile([P, GROUP * PACK], BF16, name="wc_first", align_bytes=64)
-        quantise_wc(0, wc_first[:])
-        deal_scales(uc_s, uc_s_raw)
-        make_h(0, 512, 512, gate[1], 512, nc.scalar.copy)
-        make_gates(1, 512)
-        make_h_in_place(1, 0, 256, gate[0], 0)
-        deal_uc(0)
-        quantise_wc(1, gate[0][:, (PACK - 1) * S :].bitcast(BF16))
-        deal_uc(1)
-        make_h_in_place(1, 256, 512, gate[0], 256)
-        make_y(0, 0, True, True)
-        make_y(1, 0, True, True)
-        make_h(1, 768, 256, gate[0], 768, nc.vector.tensor_copy)
-        make_y(0, 1, False, False)
-        make_y(1, 1, False, False)
-        make_y(0, 2, True, False)
-        make_y(1, 2, True, False)
+            load_state(0, t)
+        load_state(1, 0)
+        load_state(1, 1)
+        load_scale_rows(uc_s_raw, uc_scales, 8)
+        load_uc(0, 0)
+        load_state(1, 2)
+        load_wc(0)
+        nc.sync.dma_start(bias[:], b.rearrange("(g p t) -> p g t", p=P, t=PACK))
+        nc.sync.dma_start(gains[:], gain.rearrange("(g p t) -> p g t", p=P, t=PACK))
+        load_state(1, 3)
+        load_uc(1, 0)
+        load_wc(1)
+        load_uc(0, 1)
+        load_uc(1, 1)
+
+        nc.vector.tensor_copy(v_s[:], tab_s[:].indirect(offsets[:]))
+        deal(wr_w[:].bitcast(U16), wr_raw[:].bitcast(U16), 8)
+        v_w[0] = keep.tile([P, BANK], U32, name="v_w0", align_bytes=64)
+        nc.vector.tensor_copy(v_w[0][:], tab_w[:].bitcast(U32).indirect(picks(0, BANK)))
+        deal(wr_s[:], wr_s_raw[:], 16)
+        v_w[1] = keep.tile([P, BANK], U32, name="v_w1", tag="late_words", align_bytes=64)
+        nc.vector.tensor_copy(v_w[1][:], tab_w[:].bitcast(U32).indirect(picks(BANK, BANK)))
+
+
+        for a in range(GROUPS):
+            for t in range(PACK):
+                make_gate(a, t, 0)
+                make_gate(a, t, BANK)
+        FIRST = 768
+        room[0, 0] = early
+        gather_state(0, 0, 0, BANK)
+        gather_state(0, 0, BANK, BANK)
+        gather_state(0, 1, 0, S)
+        gather_state(0, 2, 0, S)
+        gather_state(0, 3, 0, BANK)
+        gather_state(0, 3, BANK, BANK)
+        make_h(0, 0, BANK, on_scalar)
+        room[1, 0] = keep.tile([P, PACK * FIRST], F32, name="room_first", tag="room0", align_bytes=64)
+        gather_state(1, 0, 0, FIRST)
+        gather_state(1, 1, 0, FIRST)
+        make_h(0, BANK, BANK, on_scalar)
+        deal(uc_s[:], uc_s_raw[:], 16)
+        deal(uc_w[0][0][:], uc_raw[0][0][:], RUN)
+        gather_state(1, 2, 0, FIRST)
+        quantise_wc(0, on_scalar, "wc_bf")
+        open_sums(0, 0, 256)
+        open_sums(0, 512, 512)
+        gather_state(1, 3, 0, 256)
+        first_bf = keep.tile([P, PACK * 256], BF16, name="first_bf", tag="room1", align_bytes=64)
+        make_h(1, 0, 256, on_scalar, first_bf)
+        deal(uc_w[1][0][:], uc_raw[1][0][:], RUN)
+        gather_state(1, 3, 256, 256)
+        make_h(1, 256, 256, on_scalar)
+        make_y(0, 0, 256, 4, 2)
+        gather_state(1, 3, 512, 256)
+        make_h(1, 512, 256, on_vector)
+        quantise_wc(1, on_vector, "room1")
+        deal(uc_w[0][1][:], uc_raw[0][1][:], RUN)
+        deal(uc_w[1][1][:], uc_raw[1][1][:], RUN)
+        make_y(0, 256, 256, 4, 2)
+        room[1, FIRST] = keep.tile([P, PACK * (S - FIRST)], F32, name="room_late", tag="room1", align_bytes=64)
+        for t in range(PACK):
+            gather_state(1, t, FIRST, S - FIRST)
+        make_h(1, 768, 256, on_vector)
+        make_y(1, 0, 512, 0, 2)
+        make_y(0, 512, 512, 0, 2)
+        make_y(1, 512, 512, 0, 2)
+        held_bf = keep.tile([P, PACK * BANK], BF16, name="held_bf", tag="room1", align_bytes=64)
+        make_planes(0, 0, 512, on_vector, held_bf)
+        make_planes(1, 0, 512, on_vector)
+        last_bf = keep.tile([P, PACK * BANK], BF16, name="last_bf", tag="after_tanh", align_bytes=64)
+        make_planes(0, 512, 512, on_scalar, last_bf)
+        make_planes(1, 512, 256, on_vector)
+        make_planes(1, 768, 256, on_scalar)
         for q in range(QUADS):
             nc.sync.dma_start(out_2[:, 4 * q : 4 * q + 4, :].bitcast(I32), y_s[32 * q : 32 * q + 8, :].bitcast(I32))

@@ -22,6 +22,7 @@ GROUP = P * PACK
 GROUPS = H // GROUP
 QUADS = 4
 RUN = 4
+PAIR = 2
 BANK = 512
 
 
@@ -125,8 +126,8 @@ def tile_list_gru_token_candidate_kernel(
 
         def weave(copy, woven, planar):
             copy(
-                out=woven.rearrange("p (c i t) -> p c t i", t=PACK, i=RUN),
-                in_=planar.rearrange("p t (c i) -> p c t i", i=RUN),
+                out=woven.rearrange("p (c i t) -> p c t i", t=PACK, i=PAIR),
+                in_=planar.rearrange("p t (c i) -> p c t i", i=PAIR),
             )
 
         def make_h(a, j0, n, copy, h_bf=None):
@@ -227,10 +228,10 @@ def tile_list_gru_token_candidate_kernel(
         load_uc(0, 0)
         load_state(1, 2)
         load_wc(0)
-        nc.sync.dma_start(bias[:], b.rearrange("(g p t) -> p g t", p=P, t=PACK))
-        nc.sync.dma_start(gains[:], gain.rearrange("(g p t) -> p g t", p=P, t=PACK))
         load_state(1, 3)
         load_uc(1, 0)
+        nc.sync.dma_start(bias[:], b.rearrange("(g p t) -> p g t", p=P, t=PACK))
+        nc.sync.dma_start(gains[:], gain.rearrange("(g p t) -> p g t", p=P, t=PACK))
         load_wc(1)
         load_uc(0, 1)
         load_uc(1, 1)

@@ -138,12 +138,15 @@ def tile_list_gru_token_candidate_kernel(
                 out=h_w[a][:, j0 : j0 + n].bitcast(FP8X4), scales=h_s[a][:, j0 : j0 + n], in_=h_bf[:, : PACK * n]
             )
 
-        def quantise_wc(g, copy, tag):
+        def weave_wc(g, copy, tag):
             wc_bf = keep.tile([P, PACK * GROUP], BF16, name="wc_bf%d" % g, tag=tag, align_bytes=64)
             copy(
-                out=wc_bf[:].rearrange("p (t m j) -> p m t j", t=PACK, j=PACK),
-                in_=wc_raw[g][:].rearrange("p j (m t) -> p m t j", t=PACK),
+                out=wc_bf[:].rearrange("p (t m j) -> p m j t", t=PACK, j=PACK),
+                in_=wc_raw[g][:].rearrange("p j (m t) -> p m j t", t=PACK),
             )
+            return wc_bf
+
+        def quantise_wc(g, wc_bf):
             nc.vector.quantize_mx(out=wc_codes[g][:].bitcast(FP8X4), scales=wc_s[g][:], in_=wc_bf[:])
 
         y_rows = {}
@@ -171,23 +174,25 @@ def tile_list_gru_token_candidate_kernel(
                     stop=(k == 2),
                 )
 
-        def make_y(g, j0, n, scalar_gains, stores):
+        def make_y(g, j0, n, scalar_gains):
             if j0 % BANK == 0:
                 y_rows[g, j0 // BANK] = rows_tile("y%d_%d" % (g, j0), [P, PACK * BANK])
             y = y_rows[g, j0 // BANK][:].rearrange("p (t j) -> p t j", t=PACK)[:, :, j0 % BANK : j0 % BANK + n]
             rows = out_0[GROUP * g : GROUP * (g + 1), j0 : j0 + n].rearrange("(p t) j -> p t j", t=PACK)
-            for t in range(PACK):
-                for k in range(2 if (g, j0, t) in sums else 0, 3):
-                    add_pass(g, j0, n, k, [t])
-                row = y[:, t, :]
-                nc.scalar.activation(out=row, in_=sums[g, j0, t][:, :n], func=ACT.Tanh, bias=bias[:, g, t : t + 1])
-                if t < scalar_gains:
-                    nc.scalar.activation(out=row, in_=row, func=ACT.Copy, scale=gains[:, g, t : t + 1])
-                else:
-                    nc.vector.tensor_scalar(out=row, in0=row, scalar1=gains[:, g, t : t + 1], scalar2=None, op0=MULT)
-                each = PACK // stores
-                if (t + 1) % each == 0:
-                    nc.sync.dma_start(rows[:, t + 1 - each : t + 1, :], y[:, t + 1 - each : t + 1, :])
+            for pair in range(0, PACK, 2):
+                for t in (pair, pair + 1):
+                    for k in range(2 if (g, j0, t) in sums else 0, 3):
+                        add_pass(g, j0, n, k, [t])
+                    nc.scalar.activation(
+                        out=y[:, t, :], in_=sums[g, j0, t][:, :n], func=ACT.Tanh, bias=bias[:, g, t : t + 1]
+                    )
+                for t in (pair, pair + 1):
+                    row = y[:, t, :]
+                    if t < scalar_gains:
+                        nc.scalar.activation(out=row, in_=row, func=ACT.Copy, scale=gains[:, g, t : t + 1])
+                    else:
+                        nc.vector.tensor_scalar(out=row, in0=row, scalar1=gains[:, g, t : t + 1], scalar2=None, op0=MULT)
+                nc.sync.dma_start(rows[:, pair : pair + 2, :], y[:, pair : pair + 2, :])
 
         def open_sums(g, j0, n):
             add_pass(g, j0, n, 0)
@@ -265,7 +270,7 @@ def tile_list_gru_token_candidate_kernel(
         deal(uc_s[:], uc_s_raw[:], 16)
         deal(uc_w[0][0][:], uc_raw[0][0][:], RUN)
         gather_state(1, 2, 0, FIRST)
-        quantise_wc(0, on_scalar, "wc_bf")
+        quantise_wc(0, weave_wc(0, on_scalar, "wc_bf"))
         open_sums(0, 0, 256)
         open_sums(0, 512, 512)
         gather_state(1, 3, 0, 256)
@@ -274,20 +279,22 @@ def tile_list_gru_token_candidate_kernel(
         deal(uc_w[1][0][:], uc_raw[1][0][:], RUN)
         gather_state(1, 3, 256, 256)
         make_h(1, 256, 256, on_scalar)
-        make_y(0, 0, 256, 4, 2)
+        make_y(0, 0, 256, 4)
         gather_state(1, 3, 512, 256)
-        make_h(1, 512, 256, on_vector)
-        quantise_wc(1, on_vector, "room1")
+        third_bf = keep.tile([P, PACK * 256], BF16, name="third_bf", tag="room1", align_bytes=64)
+        make_h(1, 512, 256, on_vector, third_bf)
+        late_wc = weave_wc(1, on_vector, "room1")
         deal(uc_w[0][1][:], uc_raw[0][1][:], RUN)
         deal(uc_w[1][1][:], uc_raw[1][1][:], RUN)
-        make_y(0, 256, 256, 4, 2)
+        quantise_wc(1, late_wc)
+        make_y(0, 256, 256, 4)
         room[1, FIRST] = keep.tile([P, PACK * (S - FIRST)], F32, name="room_late", tag="room1", align_bytes=64)
         for t in range(PACK):
             gather_state(1, t, FIRST, S - FIRST)
         make_h(1, 768, 256, on_vector)
-        make_y(1, 0, 512, 0, 2)
-        make_y(0, 512, 512, 0, 2)
-        make_y(1, 512, 512, 0, 2)
+        make_y(1, 0, 512, 0)
+        make_y(0, 512, 512, 0)
+        make_y(1, 512, 512, 0)
         held_bf = keep.tile([P, PACK * BANK], BF16, name="held_bf", tag="room1", align_bytes=64)
         make_planes(0, 0, 512, on_vector, held_bf)
         make_planes(1, 0, 512, on_vector)

@@ -21,7 +21,6 @@ PACK = 4
 GROUP = P * PACK
 GROUPS = H // GROUP
 QUADS = 4
-RUN = 4
 PAIR = 2
 BANK = 512
 
@@ -87,6 +86,12 @@ def tile_list_gru_token_candidate_kernel(
             nc.vector.tensor_copy(
                 out=dst.rearrange("p (t c i) -> p c t i", t=PACK, i=run),
                 in_=src.rearrange("p (c i t) -> p c t i", t=PACK, i=run),
+            )
+
+        def deal_words(dst, src):
+            nc.vector.tensor_copy(
+                out=dst.rearrange("p (t m) -> p m t", t=PACK),
+                in_=src.rearrange("p (m t) -> p m t", t=PACK),
             )
 
         def picks(j0, n):
@@ -213,7 +218,7 @@ def tile_list_gru_token_candidate_kernel(
         on_vector = nc.vector.tensor_copy
 
 
-        nc.gpsimd.memset(tab_s[:].bitcast(I32), 0)
+        nc.vector.memset(tab_s[:].bitcast(I32), 0)
         nc.vector.memset(wr_s_raw[:].bitcast(I32), 0)
         nc.gpsimd.memset(uc_s_raw[:].bitcast(I32), 0)
         warm = keep.tile([P, 2], F32, name="warm")
@@ -268,7 +273,7 @@ def tile_list_gru_token_candidate_kernel(
         gather_state(1, 1, 0, FIRST)
         make_h(0, BANK, BANK, on_scalar)
         deal(uc_s[:], uc_s_raw[:], 16)
-        deal(uc_w[0][0][:], uc_raw[0][0][:], RUN)
+        deal_words(uc_w[0][0][:], uc_raw[0][0][:])
         gather_state(1, 2, 0, FIRST)
         quantise_wc(0, weave_wc(0, on_scalar, "wc_bf"))
         open_sums(0, 0, 256)
@@ -276,7 +281,7 @@ def tile_list_gru_token_candidate_kernel(
         gather_state(1, 3, 0, 256)
         first_bf = keep.tile([P, PACK * 256], BF16, name="first_bf", tag="room1", align_bytes=64)
         make_h(1, 0, 256, on_scalar, first_bf)
-        deal(uc_w[1][0][:], uc_raw[1][0][:], RUN)
+        deal_words(uc_w[1][0][:], uc_raw[1][0][:])
         gather_state(1, 3, 256, 256)
         make_h(1, 256, 256, on_scalar)
         make_y(0, 0, 256, 4)
@@ -284,8 +289,8 @@ def tile_list_gru_token_candidate_kernel(
         third_bf = keep.tile([P, PACK * 256], BF16, name="third_bf", tag="room1", align_bytes=64)
         make_h(1, 512, 256, on_vector, third_bf)
         late_wc = weave_wc(1, on_vector, "room1")
-        deal(uc_w[0][1][:], uc_raw[0][1][:], RUN)
-        deal(uc_w[1][1][:], uc_raw[1][1][:], RUN)
+        deal_words(uc_w[0][1][:], uc_raw[0][1][:])
+        deal_words(uc_w[1][1][:], uc_raw[1][1][:])
         quantise_wc(1, late_wc)
         make_y(0, 256, 256, 4)
         room[1, FIRST] = keep.tile([P, PACK * (S - FIRST)], F32, name="room_late", tag="room1", align_bytes=64)

@@ -21,8 +21,14 @@ PACK = 4
 GROUP = P * PACK
 GROUPS = H // GROUP
 QUADS = 4
+SCALE_ROWS = 4
+LINE = 16
 PAIR = 2
 BANK = 512
+SLICE = 256
+FIRST = 768
+ROW_TILES = 9
+PASSES = 3
 
 
 def tile_list_gru_token_candidate_kernel(
@@ -35,7 +41,7 @@ def tile_list_gru_token_candidate_kernel(
         psum = ctx.enter_context(tc.psum_pool(name="psum", bufs=8))
 
         def rows_tile(name, shape):
-            return ring.tile(shape, F32, name=name, tag="rows", bufs=10)
+            return ring.tile(shape, F32, name=name, tag="rows", bufs=ROW_TILES)
 
         offsets = keep.tile([P, S // 16], U16, name="offsets")
         tab_s = keep.tile([P, T], U8, name="tab_s", align_bytes=64)
@@ -48,50 +54,65 @@ def tile_list_gru_token_candidate_kernel(
         uc_s = keep.tile([P, H], U8, name="uc_s", align_bytes=64)
         wc_codes = [keep.tile([P, GROUP], U32, name="wc_codes%d" % g, align_bytes=64) for g in range(GROUPS)]
         wc_s = [keep.tile([P, GROUP], U8, name="wc_s%d" % g, align_bytes=64) for g in range(GROUPS)]
-        uc_w = [[keep.tile([P, GROUP], I32, name="uc_w%d_%d" % (a, g), align_bytes=64) for g in range(GROUPS)] for a in range(GROUPS)]
-        uc_raw = [[keep.tile([P, GROUP], I32, name="uc_raw%d_%d" % (a, g)) for g in range(GROUPS)] for a in range(GROUPS)]
+        uc_w = [
+            [keep.tile([P, GROUP], I32, name="uc_w%d_%d" % (a, g), align_bytes=64) for g in range(GROUPS)]
+            for a in range(GROUPS)
+        ]
+        uc_raw = [
+            [keep.tile([P, GROUP], I32, name="uc_raw%d_%d" % (a, g)) for g in range(GROUPS)] for a in range(GROUPS)
+        ]
         bias = keep.tile([P, GROUPS, PACK], F32, name="bias", tag="after_tanh", align_bytes=64)
         gains = keep.tile([P, GROUPS, PACK], F32, name="gains")
         v_w = {}
         v_s = keep.tile([P, S], U8, name="v_s", align_bytes=64)
-        gate_pairs = [keep.tile([P, 2, S], F32, name="gate0_%d" % u, tag="room%d" % u, align_bytes=64) for u in range(2)]
+        gate_pairs = [
+            keep.tile([P, 2, S], F32, name="gate0_%d" % u, tag="room%d" % u, align_bytes=64) for u in range(2)
+        ]
         gate = {(0, t): gate_pairs[t // 2][:, t % 2, :] for t in range(PACK)}
         for t in range(PACK):
             gate[1, t] = keep.tile([P, S], F32, name="gate1_%d" % t)[:]
-        early = keep.tile([P, PACK * S], F32, name="early")
+        h_rows = {(0, 0): keep.tile([P, PACK * S], F32, name="early")}
         h_w = [keep.tile([P, S], U32, name="h_w%d" % a, align_bytes=64) for a in range(GROUPS)]
         h_s = [keep.tile([P, S], U8, name="h_s%d" % a, align_bytes=64) for a in range(GROUPS)]
         y_s = keep.tile([P, S], U8, name="y_s", align_bytes=64)
         state = {}
         wc_raw = {}
+        y_rows = {}
+        sums = {}
 
-        def load_scale_rows(plane, rows, count):
+        on_scalar = nc.scalar.copy
+        on_vector = nc.vector.tensor_copy
+
+        def load_scale_rows(tile, rows, passes):
             for q in range(QUADS):
-                nc.sync.dma_start(plane[32 * q : 32 * q + count, :].bitcast(I32), rows[:, 4 * q : 4 * q + 4, :].bitcast(I32))
+                nc.sync.dma_start(
+                    tile[32 * q : 32 * q + SCALE_ROWS * passes, :].bitcast(I32),
+                    rows[:, SCALE_ROWS * q : SCALE_ROWS * (q + 1), :].bitcast(I32),
+                )
 
         def load_state(a, t):
             state[a, t] = rows_tile("state%d_%d" % (a, t), [P, T])
             rows = gT[GROUP * a : GROUP * (a + 1), :].rearrange("(p t) w -> p t w", t=PACK)
             nc.sync.dma_start(state[a, t][:], rows[:, t, :])
 
-        def load_wc(g):
-            wc_raw[g] = rows_tile("wc_raw%d" % g, [P, PACK, GROUP])
+        def load_wc(g, tile):
+            wc_raw[g] = tile
             nc.sync.dma_start(wc_raw[g][:], wc[:, GROUP * g : GROUP * (g + 1)].rearrange("(p j) n -> p j n", j=PACK))
 
         def load_uc(a, g):
             cols = slice(GROUP * g, GROUP * (g + 1))
             nc.sync.dma_start(uc_raw[a][g][:], uc_words[a, :, cols, :].rearrange("p e i -> p (e i)").bitcast(I32))
 
-        def deal(dst, src, run):
+        def deal_narrow(dst, src, size):
             nc.vector.tensor_copy(
-                out=dst.rearrange("p (t c i) -> p c t i", t=PACK, i=run),
-                in_=src.rearrange("p (c i t) -> p c t i", t=PACK, i=run),
+                out=dst.rearrange("p (t c i) -> p c t i", t=PACK, i=LINE // size),
+                in_=src.rearrange("p (c i t) -> p c t i", t=PACK, i=LINE // size),
             )
 
-        def deal_words(dst, src):
+        def deal_uc(a, g):
             nc.vector.tensor_copy(
-                out=dst.rearrange("p (t m) -> p m t", t=PACK),
-                in_=src.rearrange("p (m t) -> p m t", t=PACK),
+                out=uc_w[a][g][:].rearrange("p (t m) -> p m t", t=PACK),
+                in_=uc_raw[a][g][:].rearrange("p (m t) -> p m t", t=PACK),
             )
 
         def picks(j0, n):
@@ -114,16 +135,14 @@ def tile_list_gru_token_candidate_kernel(
             )
             nc.scalar.activation(out=gate[a, t][:, j0 : j0 + BANK], in_=acc[:], func=ACT.Sigmoid)
 
-        room = {}
-
-        def gated(a, j0, n):
-            first = FIRST if (a, j0 >= FIRST) == (1, True) else 0
-            rows = room[a, first][:].rearrange("p (t w) -> p t w", t=PACK)
+        def h_planes(a, j0, n):
+            first = FIRST if a == 1 and j0 >= FIRST else 0
+            rows = h_rows[a, first][:].rearrange("p (t w) -> p t w", t=PACK)
             return rows[:, :, j0 - first : j0 - first + n]
 
         def gather_state(a, t, j0, n):
             nc.vector.tensor_tensor(
-                gated(a, j0, n)[:, t, :],
+                h_planes(a, j0, n)[:, t, :],
                 state[a, t][:].indirect(picks(j0, n)),
                 gate[a, t][:, j0 : j0 + n],
                 MULT,
@@ -135,10 +154,10 @@ def tile_list_gru_token_candidate_kernel(
                 in_=planar.rearrange("p t (c i) -> p c t i", i=PAIR),
             )
 
-        def make_h(a, j0, n, copy, h_bf=None):
+        def quantise_h(a, j0, n, copy, h_bf=None):
             if h_bf is None:
                 h_bf = ring.tile([P, PACK * BANK], BF16, name="h_bf", align_bytes=64, bufs=3)
-            weave(copy, h_bf[:, : PACK * n], gated(a, j0, n))
+            weave(copy, h_bf[:, : PACK * n], h_planes(a, j0, n))
             nc.vector.quantize_mx(
                 out=h_w[a][:, j0 : j0 + n].bitcast(FP8X4), scales=h_s[a][:, j0 : j0 + n], in_=h_bf[:, : PACK * n]
             )
@@ -154,40 +173,45 @@ def tile_list_gru_token_candidate_kernel(
         def quantise_wc(g, wc_bf):
             nc.vector.quantize_mx(out=wc_codes[g][:].bitcast(FP8X4), scales=wc_s[g][:], in_=wc_bf[:])
 
-        y_rows = {}
-
-        sums = {}
-
-        def add_pass(g, j0, n, k, planes=range(PACK)):
+        def add_pass(g, j0, n, t, k):
+            if k == 0:
+                sums[g, j0, t] = psum.tile([P, BANK], F32, name="acc")
+            own = slice(t * P, (t + 1) * P)
+            cols = slice(j0, j0 + n)
             at = j0 % BANK
-            for t in planes:
-                if k == 0:
-                    sums[g, j0, t] = psum.tile([P, BANK], F32, name="acc")
-                own = slice(t * P, (t + 1) * P)
-                w, w_scale, x, x_scale = [
-                    (uc_w[0][g][:, own], uc_s[:, dealt(g, t)], h_w[0][:, j0 : j0 + n], h_s[0][:, j0 : j0 + n]),
-                    (wc_codes[g][:, own], wc_s[g][:, own], v_w[j0 // BANK][:, at : at + n], v_s[:, j0 : j0 + n]),
-                    (uc_w[1][g][:, own], uc_s[4:, dealt(g, t)], h_w[1][:, j0 : j0 + n], h_s[1][:, j0 : j0 + n]),
-                ][k]
-                nc.tensor.matmul_mx(
-                    out=sums[g, j0, t][:, :n],
-                    lhsT=w.bitcast(FP8X4),
-                    lhsT_scale=w_scale,
-                    rhs=x.bitcast(FP8X4),
-                    rhs_scale=x_scale,
-                    start=(k == 0),
-                    stop=(k == 2),
-                )
+            w, w_scale, x, x_scale = [
+                (uc_w[0][g][:, own], uc_s[:, dealt(g, t)], h_w[0][:, cols], h_s[0][:, cols]),
+                (wc_codes[g][:, own], wc_s[g][:, own], v_w[j0 // BANK][:, at : at + n], v_s[:, cols]),
+                (uc_w[1][g][:, own], uc_s[SCALE_ROWS:, dealt(g, t)], h_w[1][:, cols], h_s[1][:, cols]),
+            ][k]
+            nc.tensor.matmul_mx(
+                out=sums[g, j0, t][:, :n],
+                lhsT=w.bitcast(FP8X4),
+                lhsT_scale=w_scale,
+                rhs=x.bitcast(FP8X4),
+                rhs_scale=x_scale,
+                start=(k == 0),
+                stop=(k == PASSES - 1),
+            )
+
+        def open_sums(g, j0, n):
+            for k in range(PASSES - 1):
+                for t in range(PACK):
+                    add_pass(g, j0, n, t, k)
+
+        def y_planes(g, j0, n):
+            rows = y_rows[g, j0 // BANK][:].rearrange("p (t j) -> p t j", t=PACK)
+            return rows[:, :, j0 % BANK : j0 % BANK + n]
 
         def make_y(g, j0, n, scalar_gains):
             if j0 % BANK == 0:
                 y_rows[g, j0 // BANK] = rows_tile("y%d_%d" % (g, j0), [P, PACK * BANK])
-            y = y_rows[g, j0 // BANK][:].rearrange("p (t j) -> p t j", t=PACK)[:, :, j0 % BANK : j0 % BANK + n]
+            y = y_planes(g, j0, n)
             rows = out_0[GROUP * g : GROUP * (g + 1), j0 : j0 + n].rearrange("(p t) j -> p t j", t=PACK)
             for pair in range(0, PACK, 2):
                 for t in (pair, pair + 1):
-                    for k in range(2 if (g, j0, t) in sums else 0, 3):
-                        add_pass(g, j0, n, k, [t])
+                    for k in range(PASSES - 1 if (g, j0, t) in sums else 0, PASSES):
+                        add_pass(g, j0, n, t, k)
                     nc.scalar.activation(
                         out=y[:, t, :], in_=sums[g, j0, t][:, :n], func=ACT.Tanh, bias=bias[:, g, t : t + 1]
                     )
@@ -199,24 +223,17 @@ def tile_list_gru_token_candidate_kernel(
                         nc.vector.tensor_scalar(out=row, in0=row, scalar1=gains[:, g, t : t + 1], scalar2=None, op0=MULT)
                 nc.sync.dma_start(rows[:, pair : pair + 2, :], y[:, pair : pair + 2, :])
 
-        def open_sums(g, j0, n):
-            add_pass(g, j0, n, 0)
-            add_pass(g, j0, n, 1)
-
-        def make_planes(g, j0, n, copy, y_bf=None):
-            planar = y_rows[g, j0 // BANK][:].rearrange("p (t j) -> p t j", t=PACK)[:, :, j0 % BANK : j0 % BANK + n]
+        def quantise_y(g, j0, n, copy, y_bf=None):
             if y_bf is None:
                 y_bf = ring.tile([P, PACK * BANK], BF16, name="y_bf", align_bytes=64, bufs=3)
-            weave(copy, y_bf[:, : PACK * n], planar)
+            weave(copy, y_bf[:, : PACK * n], y_planes(g, j0, n))
             y_w = keep.tile([P, n], U32, name="y_w%d_%d" % (g, j0), align_bytes=64)
-            nc.vector.quantize_mx(out=y_w[:].bitcast(FP8X4), scales=y_s[4 * g :, j0 : j0 + n], in_=y_bf[:, : PACK * n])
+            nc.vector.quantize_mx(
+                out=y_w[:].bitcast(FP8X4), scales=y_s[SCALE_ROWS * g :, j0 : j0 + n], in_=y_bf[:, : PACK * n]
+            )
             nc.sync.dma_start(
                 out_1[g, :, j0 : j0 + n, :].rearrange("p m t -> p (m t)").bitcast(I32), y_w[:].bitcast(I32)
             )
-
-        on_scalar = nc.scalar.copy
-        on_vector = nc.vector.tensor_copy
-
 
         nc.vector.memset(tab_s[:].bitcast(I32), 0)
         nc.vector.memset(wr_s_raw[:].bitcast(I32), 0)
@@ -226,86 +243,91 @@ def tile_list_gru_token_candidate_kernel(
         nc.scalar.activation(out=warm[:, 1:2], in_=warm[:, 0:1], func=ACT.Sigmoid)
 
         nc.sync.dma_start(offsets[:], offs)
-        load_scale_rows(tab_s, tab_scales, 4)
+        load_scale_rows(tab_s, tab_scales, 1)
         nc.sync.dma_start(wr_raw[:].bitcast(I32), wr_words[0].bitcast(I32))
         nc.sync.dma_start(tab_w[:], tab_words[0].rearrange("p t i -> p (t i)").bitcast(I32))
-        load_scale_rows(wr_s_raw, wr_scales, 4)
+        load_scale_rows(wr_s_raw, wr_scales, 1)
         for t in range(PACK):
             load_state(0, t)
         load_state(1, 0)
         load_state(1, 1)
-        load_scale_rows(uc_s_raw, uc_scales, 8)
+        load_scale_rows(uc_s_raw, uc_scales, GROUPS)
         load_uc(0, 0)
         load_state(1, 2)
-        load_wc(0)
+        load_wc(0, rows_tile("wc_raw0", [P, PACK, GROUP]))
         load_state(1, 3)
         load_uc(1, 0)
         nc.sync.dma_start(bias[:], b.rearrange("(g p t) -> p g t", p=P, t=PACK))
         nc.sync.dma_start(gains[:], gain.rearrange("(g p t) -> p g t", p=P, t=PACK))
-        load_wc(1)
+        load_wc(1, keep.tile([P, PACK, GROUP], F32, name="wc_raw1", tag="late_rows", align_bytes=64))
         load_uc(0, 1)
         load_uc(1, 1)
 
         nc.vector.tensor_copy(v_s[:], tab_s[:].indirect(offsets[:]))
-        deal(wr_w[:].bitcast(U16), wr_raw[:].bitcast(U16), 8)
+        deal_narrow(wr_w[:].bitcast(U16), wr_raw[:].bitcast(U16), 2)
         v_w[0] = keep.tile([P, BANK], U32, name="v_w0", align_bytes=64)
         nc.vector.tensor_copy(v_w[0][:], tab_w[:].bitcast(U32).indirect(picks(0, BANK)))
-        deal(wr_s[:], wr_s_raw[:], 16)
+        deal_narrow(wr_s[:], wr_s_raw[:], 1)
         v_w[1] = keep.tile([P, BANK], U32, name="v_w1", tag="late_words", align_bytes=64)
         nc.vector.tensor_copy(v_w[1][:], tab_w[:].bitcast(U32).indirect(picks(BANK, BANK)))
-
 
         for a in range(GROUPS):
             for t in range(PACK):
                 make_gate(a, t, 0)
                 make_gate(a, t, BANK)
-        FIRST = 768
-        room[0, 0] = early
-        gather_state(0, 0, 0, BANK)
-        gather_state(0, 0, BANK, BANK)
-        gather_state(0, 1, 0, S)
-        gather_state(0, 2, 0, S)
-        gather_state(0, 3, 0, BANK)
-        gather_state(0, 3, BANK, BANK)
-        make_h(0, 0, BANK, on_scalar)
-        room[1, 0] = keep.tile([P, PACK * FIRST], F32, name="room_first", tag="room0", align_bytes=64)
+
+        for t in range(PACK):
+            width = BANK if t in (0, PACK - 1) else S
+            for j0 in range(0, S, width):
+                gather_state(0, t, j0, width)
+        quantise_h(0, 0, BANK, on_scalar)
+
+        h_rows[1, 0] = keep.tile([P, PACK * FIRST], F32, name="room_first", tag="room0", align_bytes=64)
         gather_state(1, 0, 0, FIRST)
         gather_state(1, 1, 0, FIRST)
-        make_h(0, BANK, BANK, on_scalar)
-        deal(uc_s[:], uc_s_raw[:], 16)
-        deal_words(uc_w[0][0][:], uc_raw[0][0][:])
+        quantise_h(0, BANK, BANK, on_scalar)
+        deal_narrow(uc_s[:], uc_s_raw[:], 1)
+        deal_uc(0, 0)
         gather_state(1, 2, 0, FIRST)
         quantise_wc(0, weave_wc(0, on_scalar, "wc_bf"))
-        open_sums(0, 0, 256)
-        open_sums(0, 512, 512)
-        gather_state(1, 3, 0, 256)
-        first_bf = keep.tile([P, PACK * 256], BF16, name="first_bf", tag="room1", align_bytes=64)
-        make_h(1, 0, 256, on_scalar, first_bf)
-        deal_words(uc_w[1][0][:], uc_raw[1][0][:])
-        gather_state(1, 3, 256, 256)
-        make_h(1, 256, 256, on_scalar)
-        make_y(0, 0, 256, 4)
-        gather_state(1, 3, 512, 256)
-        third_bf = keep.tile([P, PACK * 256], BF16, name="third_bf", tag="room1", align_bytes=64)
-        make_h(1, 512, 256, on_vector, third_bf)
-        late_wc = weave_wc(1, on_vector, "room1")
-        deal_words(uc_w[0][1][:], uc_raw[0][1][:])
-        deal_words(uc_w[1][1][:], uc_raw[1][1][:])
+        open_sums(0, 0, SLICE)
+        open_sums(0, BANK, BANK)
+
+        last = PACK - 1
+        gather_state(1, last, 0, SLICE)
+        first_bf = keep.tile([P, PACK * SLICE], BF16, name="first_bf", tag="room1", align_bytes=64)
+        quantise_h(1, 0, SLICE, on_scalar, first_bf)
+        deal_uc(1, 0)
+        gather_state(1, last, SLICE, SLICE)
+        second_bf = keep.tile([P, PACK * SLICE], BF16, name="second_bf", tag="late_wc", align_bytes=64)
+        quantise_h(1, SLICE, SLICE, on_scalar, second_bf)
+        make_y(0, 0, SLICE, PACK)
+        gather_state(1, last, BANK, SLICE)
+        third_bf = keep.tile([P, PACK * SLICE], BF16, name="third_bf", tag="room1", align_bytes=64)
+        quantise_h(1, BANK, SLICE, on_vector, third_bf)
+        late_wc = weave_wc(1, on_vector, "late_wc")
+        deal_uc(0, 1)
+        deal_uc(1, 1)
         quantise_wc(1, late_wc)
-        make_y(0, 256, 256, 4)
-        room[1, FIRST] = keep.tile([P, PACK * (S - FIRST)], F32, name="room_late", tag="room1", align_bytes=64)
+        make_y(0, SLICE, SLICE, PACK)
+        h_rows[1, FIRST] = keep.tile([P, PACK * (S - FIRST)], F32, name="room_late", tag="late_rows", align_bytes=64)
         for t in range(PACK):
             gather_state(1, t, FIRST, S - FIRST)
-        make_h(1, 768, 256, on_vector)
-        make_y(1, 0, 512, 0)
-        make_y(0, 512, 512, 0)
-        make_y(1, 512, 512, 0)
-        held_bf = keep.tile([P, PACK * BANK], BF16, name="held_bf", tag="room1", align_bytes=64)
-        make_planes(0, 0, 512, on_vector, held_bf)
-        make_planes(1, 0, 512, on_vector)
+        quantise_h(1, FIRST, S - FIRST, on_vector)
+
+        make_y(1, 0, BANK, 0)
+        make_y(0, BANK, BANK, 0)
+        make_y(1, BANK, BANK, 0)
+
+        held_bf = keep.tile([P, PACK * BANK], BF16, name="held_bf", tag="late_rows", align_bytes=64)
+        quantise_y(0, 0, BANK, on_vector, held_bf)
+        quantise_y(1, 0, BANK, on_vector)
         last_bf = keep.tile([P, PACK * BANK], BF16, name="last_bf", tag="after_tanh", align_bytes=64)
-        make_planes(0, 512, 512, on_scalar, last_bf)
-        make_planes(1, 512, 256, on_vector)
-        make_planes(1, 768, 256, on_scalar)
+        quantise_y(0, BANK, BANK, on_scalar, last_bf)
+        quantise_y(1, BANK, SLICE, on_vector)
+        quantise_y(1, BANK + SLICE, SLICE, on_scalar)
         for q in range(QUADS):
-            nc.sync.dma_start(out_2[:, 4 * q : 4 * q + 4, :].bitcast(I32), y_s[32 * q : 32 * q + 8, :].bitcast(I32))
+            nc.sync.dma_start(
+                out_2[:, SCALE_ROWS * q : SCALE_ROWS * (q + 1), :].bitcast(I32),
+                y_s[32 * q : 32 * q + SCALE_ROWS * GROUPS, :].bitcast(I32),
+            )

@@ -28,7 +28,8 @@ BANK = 512
 SLICE = 256
 FIRST = 768
 ROW_TILES = 9
-PASSES = 3
+TOKEN = GROUPS
+PASSES = GROUPS + 1
 
 
 def tile_list_gru_token_candidate_kernel(
@@ -50,9 +51,9 @@ def tile_list_gru_token_candidate_kernel(
         wr_w = keep.tile([P, 2 * H], U8, name="wr_w", align_bytes=64)
         wr_s_raw = keep.tile([P, H], U8, name="wr_s_raw", tag="late_words", align_bytes=64)
         uc_s_raw = keep.tile([P, H], U8, name="uc_s_raw", align_bytes=64)
-        wr_s = keep.tile([P, H], U8, name="wr_s", align_bytes=64)
+        wr_s = [keep.tile([P, GROUP], U8, name="wr_s%d" % a, align_bytes=64) for a in range(GROUPS)]
         uc_s = keep.tile([P, H], U8, name="uc_s", align_bytes=64)
-        wc_codes = [keep.tile([P, GROUP], U32, name="wc_codes%d" % g, align_bytes=64) for g in range(GROUPS)]
+        wc_codes = {}
         wc_s = [keep.tile([P, GROUP], U8, name="wc_s%d" % g, align_bytes=64) for g in range(GROUPS)]
         uc_w = [
             [keep.tile([P, GROUP], I32, name="uc_w%d_%d" % (a, g), align_bytes=64) for g in range(GROUPS)]
@@ -69,8 +70,9 @@ def tile_list_gru_token_candidate_kernel(
             keep.tile([P, 2, S], F32, name="gate0_%d" % u, tag="room%d" % u, align_bytes=64) for u in range(2)
         ]
         gate = {(0, t): gate_pairs[t // 2][:, t % 2, :] for t in range(PACK)}
-        for t in range(PACK):
+        for t in range(PACK - 1):
             gate[1, t] = keep.tile([P, S], F32, name="gate1_%d" % t)[:]
+        last_gate = [keep.tile([P, BANK], F32, name="last_gate%d" % u, align_bytes=64)[:] for u in range(2)]
         h_rows = {(0, 0): keep.tile([P, PACK * S], F32, name="early")}
         h_w = [keep.tile([P, S], U32, name="h_w%d" % a, align_bytes=64) for a in range(GROUPS)]
         h_s = [keep.tile([P, S], U8, name="h_s%d" % a, align_bytes=64) for a in range(GROUPS)]
@@ -79,6 +81,7 @@ def tile_list_gru_token_candidate_kernel(
         wc_raw = {}
         y_rows = {}
         sums = {}
+        passes = {}
 
         on_scalar = nc.scalar.copy
         on_vector = nc.vector.tensor_copy
@@ -95,9 +98,9 @@ def tile_list_gru_token_candidate_kernel(
             rows = gT[GROUP * a : GROUP * (a + 1), :].rearrange("(p t) w -> p t w", t=PACK)
             nc.sync.dma_start(state[a, t][:], rows[:, t, :])
 
-        def load_wc(g, tile):
-            wc_raw[g] = tile
-            nc.sync.dma_start(wc_raw[g][:], wc[:, GROUP * g : GROUP * (g + 1)].rearrange("(p j) n -> p j n", j=PACK))
+        def load_wc(c0, tile):
+            wc_raw[c0] = tile
+            nc.sync.dma_start(tile[:], wc[:, c0 : c0 + tile.shape[2]].rearrange("(p j) n -> p j n", j=PACK))
 
         def load_uc(a, g):
             cols = slice(GROUP * g, GROUP * (g + 1))
@@ -121,19 +124,24 @@ def tile_list_gru_token_candidate_kernel(
         def dealt(g, t):
             return slice(t * (H // PACK) + g * P, t * (H // PACK) + (g + 1) * P)
 
+        def gates(a, t, j0, n):
+            if (a, t) == (GROUPS - 1, PACK - 1):
+                return last_gate[j0 // BANK][:, j0 % BANK : j0 % BANK + n]
+            return gate[a, t][:, j0 : j0 + n]
+
         def make_gate(a, t, j0):
             acc = psum.tile([P, BANK], F32, name="acc")
             cols = dealt(a, t)
             nc.tensor.matmul_mx(
                 out=acc[:],
                 lhsT=wr_w[:, 2 * cols.start : 2 * cols.stop].bitcast(FP4X4),
-                lhsT_scale=wr_s[:, cols],
+                lhsT_scale=wr_s[a][:, t * P : (t + 1) * P],
                 rhs=v_w[j0 // BANK][:].bitcast(FP8X4),
                 rhs_scale=v_s[:, j0 : j0 + BANK],
                 start=True,
                 stop=True,
             )
-            nc.scalar.activation(out=gate[a, t][:, j0 : j0 + BANK], in_=acc[:], func=ACT.Sigmoid)
+            nc.scalar.activation(out=gates(a, t, j0, BANK), in_=acc[:], func=ACT.Sigmoid)
 
         def h_planes(a, j0, n):
             first = FIRST if a == 1 and j0 >= FIRST else 0
@@ -144,7 +152,7 @@ def tile_list_gru_token_candidate_kernel(
             nc.vector.tensor_tensor(
                 h_planes(a, j0, n)[:, t, :],
                 state[a, t][:].indirect(picks(j0, n)),
-                gate[a, t][:, j0 : j0 + n],
+                gates(a, t, j0, n),
                 MULT,
             )
 
@@ -162,56 +170,59 @@ def tile_list_gru_token_candidate_kernel(
                 out=h_w[a][:, j0 : j0 + n].bitcast(FP8X4), scales=h_s[a][:, j0 : j0 + n], in_=h_bf[:, : PACK * n]
             )
 
-        def weave_wc(g, copy, tag):
-            wc_bf = keep.tile([P, PACK * GROUP], BF16, name="wc_bf%d" % g, tag=tag, align_bytes=64)
+        def weave_wc(c0, copy, wc_bf):
+            m0, count = c0 % GROUP // PACK, wc_raw[c0].shape[2] // PACK
             copy(
-                out=wc_bf[:].rearrange("p (t m j) -> p m j t", t=PACK, j=PACK),
-                in_=wc_raw[g][:].rearrange("p j (m t) -> p m j t", t=PACK),
+                out=wc_bf[:].rearrange("p (t m j) -> p m j t", t=PACK, j=PACK)[:, m0 : m0 + count],
+                in_=wc_raw[c0][:].rearrange("p j (m t) -> p m j t", t=PACK),
             )
-            return wc_bf
 
-        def quantise_wc(g, wc_bf):
+        def quantise_wc(g, wc_bf, tag):
+            wc_codes[g] = keep.tile([P, GROUP], U32, name="wc_codes%d" % g, tag=tag, align_bytes=64)
             nc.vector.quantize_mx(out=wc_codes[g][:].bitcast(FP8X4), scales=wc_s[g][:], in_=wc_bf[:])
 
-        def add_pass(g, j0, n, t, k):
-            if k == 0:
+        def add_pass(g, j0, n, t, term):
+            done = passes.setdefault((g, j0, t), [])
+            if not done:
                 sums[g, j0, t] = psum.tile([P, BANK], F32, name="acc")
+            done.append(term)
             own = slice(t * P, (t + 1) * P)
             cols = slice(j0, j0 + n)
-            at = j0 % BANK
-            w, w_scale, x, x_scale = [
-                (uc_w[0][g][:, own], uc_s[:, dealt(g, t)], h_w[0][:, cols], h_s[0][:, cols]),
-                (wc_codes[g][:, own], wc_s[g][:, own], v_w[j0 // BANK][:, at : at + n], v_s[:, cols]),
-                (uc_w[1][g][:, own], uc_s[SCALE_ROWS:, dealt(g, t)], h_w[1][:, cols], h_s[1][:, cols]),
-            ][k]
+            if term == TOKEN:
+                at = j0 % BANK
+                w, w_scale = wc_codes[g][:, own], wc_s[g][:, own]
+                x, x_scale = v_w[j0 // BANK][:, at : at + n], v_s[:, cols]
+            else:
+                w, w_scale = uc_w[term][g][:, own], uc_s[SCALE_ROWS * term :, dealt(g, t)]
+                x, x_scale = h_w[term][:, cols], h_s[term][:, cols]
             nc.tensor.matmul_mx(
                 out=sums[g, j0, t][:, :n],
                 lhsT=w.bitcast(FP8X4),
                 lhsT_scale=w_scale,
                 rhs=x.bitcast(FP8X4),
                 rhs_scale=x_scale,
-                start=(k == 0),
-                stop=(k == PASSES - 1),
+                start=(len(done) == 1),
+                stop=(len(done) == PASSES),
             )
 
-        def open_sums(g, j0, n):
-            for k in range(PASSES - 1):
+        def open_sums(g, j0, n, terms):
+            for term in terms:
                 for t in range(PACK):
-                    add_pass(g, j0, n, t, k)
+                    add_pass(g, j0, n, t, term)
 
         def y_planes(g, j0, n):
             rows = y_rows[g, j0 // BANK][:].rearrange("p (t j) -> p t j", t=PACK)
             return rows[:, :, j0 % BANK : j0 % BANK + n]
 
-        def make_y(g, j0, n, scalar_gains):
+        def make_y(g, j0, n, terms, scalar_gains):
             if j0 % BANK == 0:
                 y_rows[g, j0 // BANK] = rows_tile("y%d_%d" % (g, j0), [P, PACK * BANK])
             y = y_planes(g, j0, n)
             rows = out_0[GROUP * g : GROUP * (g + 1), j0 : j0 + n].rearrange("(p t) j -> p t j", t=PACK)
             for pair in range(0, PACK, 2):
                 for t in (pair, pair + 1):
-                    for k in range(PASSES - 1 if (g, j0, t) in sums else 0, PASSES):
-                        add_pass(g, j0, n, t, k)
+                    for term in terms:
+                        add_pass(g, j0, n, t, term)
                     nc.scalar.activation(
                         out=y[:, t, :], in_=sums[g, j0, t][:, :n], func=ACT.Tanh, bias=bias[:, g, t : t + 1]
                     )
@@ -243,8 +254,9 @@ def tile_list_gru_token_candidate_kernel(
         nc.scalar.activation(out=warm[:, 1:2], in_=warm[:, 0:1], func=ACT.Sigmoid)
 
         nc.sync.dma_start(offsets[:], offs)
-        load_scale_rows(tab_s, tab_scales, 1)
         nc.sync.dma_start(wr_raw[:].bitcast(I32), wr_words[0].bitcast(I32))
+        load_uc(0, 0)
+        load_scale_rows(tab_s, tab_scales, 1)
         nc.sync.dma_start(tab_w[:], tab_words[0].rearrange("p t i -> p (t i)").bitcast(I32))
         load_scale_rows(wr_s_raw, wr_scales, 1)
         for t in range(PACK):
@@ -252,22 +264,23 @@ def tile_list_gru_token_candidate_kernel(
         load_state(1, 0)
         load_state(1, 1)
         load_scale_rows(uc_s_raw, uc_scales, GROUPS)
-        load_uc(0, 0)
         load_state(1, 2)
         load_wc(0, rows_tile("wc_raw0", [P, PACK, GROUP]))
+        load_wc(GROUP, keep.tile([P, PACK, SLICE], F32, name="wc_raw_third", align_bytes=64))
         load_state(1, 3)
         load_uc(1, 0)
         nc.sync.dma_start(bias[:], b.rearrange("(g p t) -> p g t", p=P, t=PACK))
         nc.sync.dma_start(gains[:], gain.rearrange("(g p t) -> p g t", p=P, t=PACK))
-        load_wc(1, keep.tile([P, PACK, GROUP], F32, name="wc_raw1", tag="late_rows", align_bytes=64))
         load_uc(0, 1)
+        load_wc(GROUP + SLICE, keep.tile([P, PACK, SLICE], F32, name="wc_raw_last", tag="late_rows", align_bytes=64))
         load_uc(1, 1)
 
         nc.vector.tensor_copy(v_s[:], tab_s[:].indirect(offsets[:]))
         deal_narrow(wr_w[:].bitcast(U16), wr_raw[:].bitcast(U16), 2)
         v_w[0] = keep.tile([P, BANK], U32, name="v_w0", align_bytes=64)
         nc.vector.tensor_copy(v_w[0][:], tab_w[:].bitcast(U32).indirect(picks(0, BANK)))
-        deal_narrow(wr_s[:], wr_s_raw[:], 1)
+        for a in range(GROUPS):
+            deal_narrow(wr_s[a][:], wr_s_raw[:, GROUP * a : GROUP * (a + 1)], 1)
         v_w[1] = keep.tile([P, BANK], U32, name="v_w1", tag="late_words", align_bytes=64)
         nc.vector.tensor_copy(v_w[1][:], tab_w[:].bitcast(U32).indirect(picks(BANK, BANK)))
 
@@ -289,9 +302,12 @@ def tile_list_gru_token_candidate_kernel(
         deal_narrow(uc_s[:], uc_s_raw[:], 1)
         deal_uc(0, 0)
         gather_state(1, 2, 0, FIRST)
-        quantise_wc(0, weave_wc(0, on_scalar, "wc_bf"))
-        open_sums(0, 0, SLICE)
-        open_sums(0, BANK, BANK)
+        early_wc = keep.tile([P, PACK * GROUP], BF16, name="early_wc", align_bytes=64)
+        late_wc = keep.tile([P, PACK * GROUP], BF16, name="late_wc", align_bytes=64)
+        weave_wc(0, on_scalar, early_wc)
+        weave_wc(GROUP, on_scalar, late_wc)
+        open_sums(0, 0, SLICE, (0,))
+        open_sums(0, BANK, BANK, (0,))
 
         last = PACK - 1
         gather_state(1, last, 0, SLICE)
@@ -299,29 +315,34 @@ def tile_list_gru_token_candidate_kernel(
         quantise_h(1, 0, SLICE, on_scalar, first_bf)
         deal_uc(1, 0)
         gather_state(1, last, SLICE, SLICE)
-        second_bf = keep.tile([P, PACK * SLICE], BF16, name="second_bf", tag="late_wc", align_bytes=64)
+        quantise_wc(0, early_wc, "last_gate0")
+        open_sums(0, 0, SLICE, (TOKEN,))
+        second_bf = keep.tile([P, PACK * SLICE], BF16, name="second_bf", align_bytes=64)
         quantise_h(1, SLICE, SLICE, on_scalar, second_bf)
-        make_y(0, 0, SLICE, PACK)
-        gather_state(1, last, BANK, SLICE)
-        third_bf = keep.tile([P, PACK * SLICE], BF16, name="third_bf", tag="room1", align_bytes=64)
-        quantise_h(1, BANK, SLICE, on_vector, third_bf)
-        late_wc = weave_wc(1, on_vector, "late_wc")
+        make_y(0, 0, SLICE, (1,), PACK)
+        open_sums(0, BANK, BANK, (TOKEN,))
+        gather_state(1, last, BANK, FIRST - BANK)
+        third_bf = keep.tile([P, PACK * BANK], BF16, name="third_bf", tag="room1", align_bytes=64)
+        weave(on_vector, third_bf[:, : PACK * (FIRST - BANK)], h_planes(1, BANK, FIRST - BANK))
         deal_uc(0, 1)
+        weave_wc(GROUP + SLICE, on_vector, late_wc)
         deal_uc(1, 1)
-        quantise_wc(1, late_wc)
-        make_y(0, SLICE, SLICE, PACK)
+        quantise_wc(1, late_wc, "wc_codes1")
+        make_y(0, SLICE, SLICE, (0, TOKEN, 1), PACK)
         h_rows[1, FIRST] = keep.tile([P, PACK * (S - FIRST)], F32, name="room_late", tag="late_rows", align_bytes=64)
         for t in range(PACK):
             gather_state(1, t, FIRST, S - FIRST)
-        quantise_h(1, FIRST, S - FIRST, on_vector)
+        weave(on_vector, third_bf[:, PACK * (FIRST - BANK) :], h_planes(1, FIRST, S - FIRST))
+        nc.vector.quantize_mx(out=h_w[1][:, BANK:].bitcast(FP8X4), scales=h_s[1][:, BANK:], in_=third_bf[:])
 
-        make_y(1, 0, BANK, 0)
-        make_y(0, BANK, BANK, 0)
-        make_y(1, BANK, BANK, 0)
+        make_y(1, 0, BANK, (0, TOKEN, 1), 0)
+        make_y(0, BANK, BANK, (1,), 0)
+        make_y(1, BANK, BANK, (0, TOKEN, 1), 0)
 
         held_bf = keep.tile([P, PACK * BANK], BF16, name="held_bf", tag="late_rows", align_bytes=64)
-        quantise_y(0, 0, BANK, on_vector, held_bf)
-        quantise_y(1, 0, BANK, on_vector)
+        quantise_y(1, 0, BANK, on_vector, held_bf)
+        next_bf = keep.tile([P, PACK * BANK], BF16, name="next_bf", tag="late_rows", align_bytes=64)
+        quantise_y(0, 0, BANK, on_vector, next_bf)
         last_bf = keep.tile([P, PACK * BANK], BF16, name="last_bf", tag="after_tanh", align_bytes=64)
         quantise_y(0, BANK, BANK, on_scalar, last_bf)
         quantise_y(1, BANK, SLICE, on_vector)

@@ -26,8 +26,7 @@ LINE = 16
 PAIR = 2
 BANK = 512
 SLICE = 256
-FIRST = 768
-ROW_TILES = 9
+SHARE = 256
 TOKEN = GROUPS
 PASSES = GROUPS + 1
 
@@ -41,70 +40,67 @@ def tile_list_gru_token_candidate_kernel(
         ring = ctx.enter_context(tc.tile_pool(name="ring", bufs=2))
         psum = ctx.enter_context(tc.psum_pool(name="psum", bufs=8))
 
-        def rows_tile(name, shape):
-            return ring.tile(shape, F32, name=name, tag="rows", bufs=ROW_TILES)
+        def kept(name, width, dtype, tag=""):
+            return keep.tile([P, width], dtype, name=name, tag=tag, align_bytes=64)
+
+        def rows_tile(name):
+            return ring.tile([P, T], F32, name=name, tag="rows", bufs=GROUPS * PACK)
 
         offsets = keep.tile([P, S // 16], U16, name="offsets")
-        tab_s = keep.tile([P, T], U8, name="tab_s", align_bytes=64)
-        tab_w = keep.tile([P, T], I32, name="tab_w", align_bytes=64)
-        wr_raw = keep.tile([P, 2 * H], U8, name="wr_raw", align_bytes=64)
-        wr_w = keep.tile([P, 2 * H], U8, name="wr_w", align_bytes=64)
-        wr_s_raw = keep.tile([P, H], U8, name="wr_s_raw", tag="late_words", align_bytes=64)
-        uc_s_raw = keep.tile([P, H], U8, name="uc_s_raw", align_bytes=64)
-        wr_s = [keep.tile([P, GROUP], U8, name="wr_s%d" % a, align_bytes=64) for a in range(GROUPS)]
-        uc_s = keep.tile([P, H], U8, name="uc_s", align_bytes=64)
-        wc_codes = {}
-        wc_s = [keep.tile([P, GROUP], U8, name="wc_s%d" % g, align_bytes=64) for g in range(GROUPS)]
-        uc_w = [
-            [keep.tile([P, GROUP], I32, name="uc_w%d_%d" % (a, g), align_bytes=64) for g in range(GROUPS)]
-            for a in range(GROUPS)
-        ]
-        uc_raw = [
-            [keep.tile([P, GROUP], I32, name="uc_raw%d_%d" % (a, g)) for g in range(GROUPS)] for a in range(GROUPS)
-        ]
-        bias = keep.tile([P, GROUPS, PACK], F32, name="bias", tag="after_tanh", align_bytes=64)
-        gains = keep.tile([P, GROUPS, PACK], F32, name="gains")
+        tab_s = kept("tab_s", T, U8)
+        tab_w = kept("tab_w", T, I32)
+        wr_raw = kept("wr_raw", 2 * H, U8)
+        wr_w = kept("wr_w", 2 * H, U8)
+        wr_s_raw = kept("wr_s_raw", H, U8, "late_words")
+        wr_s = [kept("wr_s%d" % a, GROUP, U8) for a in range(GROUPS)]
+        uc_s_raw = kept("uc_s_raw", H, U8)
+        uc_s = kept("uc_s", H, U8)
+        uc_raw = [kept("uc_raw%d" % a, H, I32) for a in range(GROUPS)]
+        uc_w = [kept("uc_w%d" % a, H, U32) for a in range(GROUPS)]
+        wc_raw = [keep.tile([P, PACK, GROUP], F32, name="wc_raw%d" % g, align_bytes=64) for g in range(GROUPS)]
+        wc_bf = [kept("wc_bf%d" % g, PACK * GROUP, BF16) for g in range(GROUPS)]
+        wc_w = {1: kept("wc_w1", GROUP, U32)}
+        wc_s = [kept("wc_s%d" % g, GROUP, U8) for g in range(GROUPS)]
+        bias = keep.tile([P, GROUPS, PACK], F32, name="bias", align_bytes=64)
+        gains = keep.tile([P, GROUPS, PACK], F32, name="gains", align_bytes=64)
         v_w = {}
-        v_s = keep.tile([P, S], U8, name="v_s", align_bytes=64)
-        gate_pairs = [
-            keep.tile([P, 2, S], F32, name="gate0_%d" % u, tag="room%d" % u, align_bytes=64) for u in range(2)
-        ]
-        gate = {(0, t): gate_pairs[t // 2][:, t % 2, :] for t in range(PACK)}
-        for t in range(PACK - 1):
-            gate[1, t] = keep.tile([P, S], F32, name="gate1_%d" % t)[:]
-        last_gate = [keep.tile([P, BANK], F32, name="last_gate%d" % u, align_bytes=64)[:] for u in range(2)]
-        h_rows = {(0, 0): keep.tile([P, PACK * S], F32, name="early")}
-        h_w = [keep.tile([P, S], U32, name="h_w%d" % a, align_bytes=64) for a in range(GROUPS)]
-        h_s = [keep.tile([P, S], U8, name="h_s%d" % a, align_bytes=64) for a in range(GROUPS)]
-        y_s = keep.tile([P, S], U8, name="y_s", align_bytes=64)
+        v_s = kept("v_s", S, U8)
+        gate = {(a, t, 0): kept("gate%d_%d" % (a, t), S, F32) for a in range(GROUPS) for t in range(PACK - 2 * a)}
+        for piece in ((1, 2, 0), (1, 2, BANK), (1, 3, BANK)):
+            gate[piece] = kept("gate%d_%d_%d" % piece, BANK, F32)
+        h_rows = [kept("h_rows%d" % a, PACK * S, F32) for a in range(GROUPS)]
+        gate[1, 3, 0] = h_rows[1][:, 2 * S + BANK : 3 * S]
+        h_bf = {(0, 0): kept("h_bf0", PACK * S, BF16), (1, 0): kept("h_bf1", PACK * BANK, BF16)}
+        h_w = {1: kept("h_w1", S, U32)}
+        h_s = [kept("h_s%d" % a, S, U8) for a in range(GROUPS)]
+        y_w = [kept("y_w%d" % g, S, U32) for g in range(GROUPS)]
+        y_s = kept("y_s", S, U8)
         state = {}
-        wc_raw = {}
         y_rows = {}
+        y_bf = {}
         sums = {}
         passes = {}
 
         on_scalar = nc.scalar.copy
         on_vector = nc.vector.tensor_copy
 
-        def load_scale_rows(tile, rows, passes):
+        def load_scale_rows(tile, rows, count):
             for q in range(QUADS):
                 nc.sync.dma_start(
-                    tile[32 * q : 32 * q + SCALE_ROWS * passes, :].bitcast(I32),
+                    tile[32 * q : 32 * q + SCALE_ROWS * count, :].bitcast(I32),
                     rows[:, SCALE_ROWS * q : SCALE_ROWS * (q + 1), :].bitcast(I32),
                 )
 
         def load_state(a, t):
-            state[a, t] = rows_tile("state%d_%d" % (a, t), [P, T])
+            state[a, t] = rows_tile("state%d_%d" % (a, t))
             rows = gT[GROUP * a : GROUP * (a + 1), :].rearrange("(p t) w -> p t w", t=PACK)
             nc.sync.dma_start(state[a, t][:], rows[:, t, :])
 
-        def load_wc(c0, tile):
-            wc_raw[c0] = tile
-            nc.sync.dma_start(tile[:], wc[:, c0 : c0 + tile.shape[2]].rearrange("(p j) n -> p j n", j=PACK))
+        def load_wc(g):
+            nc.sync.dma_start(wc_raw[g][:], wc[:, GROUP * g : GROUP * (g + 1)].rearrange("(p j) n -> p j n", j=PACK))
 
-        def load_uc(a, g):
-            cols = slice(GROUP * g, GROUP * (g + 1))
-            nc.sync.dma_start(uc_raw[a][g][:], uc_words[a, :, cols, :].rearrange("p e i -> p (e i)").bitcast(I32))
+        def load_uc(a):
+            nc.sync.dma_start(uc_raw[a][:], uc_words[a].rearrange("p e i -> p (e i)").bitcast(I32))
 
         def deal_narrow(dst, src, size):
             nc.vector.tensor_copy(
@@ -112,10 +108,10 @@ def tile_list_gru_token_candidate_kernel(
                 in_=src.rearrange("p (c i t) -> p c t i", t=PACK, i=LINE // size),
             )
 
-        def deal_uc(a, g):
-            nc.vector.tensor_copy(
-                out=uc_w[a][g][:].rearrange("p (t m) -> p m t", t=PACK),
-                in_=uc_raw[a][g][:].rearrange("p (m t) -> p m t", t=PACK),
+        def deal_uc(a):
+            nc.scalar.copy(
+                out=uc_w[a][:].rearrange("p (t m) -> p m t", t=PACK),
+                in_=uc_raw[a][:].bitcast(U32).rearrange("p (m t) -> p m t", t=PACK),
             )
 
         def picks(j0, n):
@@ -124,10 +120,12 @@ def tile_list_gru_token_candidate_kernel(
         def dealt(g, t):
             return slice(t * (H // PACK) + g * P, t * (H // PACK) + (g + 1) * P)
 
+        def planes(rows, j0, n):
+            return rows[:].rearrange("p (t w) -> p t w", t=PACK)[:, :, j0 : j0 + n]
+
         def gates(a, t, j0, n):
-            if (a, t) == (GROUPS - 1, PACK - 1):
-                return last_gate[j0 // BANK][:, j0 % BANK : j0 % BANK + n]
-            return gate[a, t][:, j0 : j0 + n]
+            first = j0 // BANK * BANK if (a, t) >= (1, 2) else 0
+            return gate[a, t, first][:, j0 - first : j0 - first + n]
 
         def make_gate(a, t, j0):
             acc = psum.tile([P, BANK], F32, name="acc")
@@ -136,21 +134,16 @@ def tile_list_gru_token_candidate_kernel(
                 out=acc[:],
                 lhsT=wr_w[:, 2 * cols.start : 2 * cols.stop].bitcast(FP4X4),
                 lhsT_scale=wr_s[a][:, t * P : (t + 1) * P],
-                rhs=v_w[j0 // BANK][:].bitcast(FP8X4),
+                rhs=v_w[j0][:].bitcast(FP8X4),
                 rhs_scale=v_s[:, j0 : j0 + BANK],
                 start=True,
                 stop=True,
             )
             nc.scalar.activation(out=gates(a, t, j0, BANK), in_=acc[:], func=ACT.Sigmoid)
 
-        def h_planes(a, j0, n):
-            first = FIRST if a == 1 and j0 >= FIRST else 0
-            rows = h_rows[a, first][:].rearrange("p (t w) -> p t w", t=PACK)
-            return rows[:, :, j0 - first : j0 - first + n]
-
         def gather_state(a, t, j0, n):
             nc.vector.tensor_tensor(
-                h_planes(a, j0, n)[:, t, :],
+                planes(h_rows[a], j0, n)[:, t, :],
                 state[a, t][:].indirect(picks(j0, n)),
                 gates(a, t, j0, n),
                 MULT,
@@ -162,41 +155,44 @@ def tile_list_gru_token_candidate_kernel(
                 in_=planar.rearrange("p t (c i) -> p c t i", i=PAIR),
             )
 
-        def quantise_h(a, j0, n, copy, h_bf=None):
-            if h_bf is None:
-                h_bf = ring.tile([P, PACK * BANK], BF16, name="h_bf", align_bytes=64, bufs=3)
-            weave(copy, h_bf[:, : PACK * n], h_planes(a, j0, n))
+        def woven_h(a, j0, n):
+            first = j0 // BANK * BANK if a else 0
+            return h_bf[a, first][:, PACK * (j0 - first) : PACK * (j0 - first + n)]
+
+        def weave_h(a, j0, n, copy):
+            weave(copy, woven_h(a, j0, n), planes(h_rows[a], j0, n))
+
+        def quantise_h(a, j0, n):
             nc.vector.quantize_mx(
-                out=h_w[a][:, j0 : j0 + n].bitcast(FP8X4), scales=h_s[a][:, j0 : j0 + n], in_=h_bf[:, : PACK * n]
+                out=h_w[a][:, j0 : j0 + n].bitcast(FP8X4),
+                scales=h_s[a][:, j0 : j0 + n],
+                in_=woven_h(a, j0, n),
             )
 
-        def weave_wc(c0, copy, wc_bf):
-            m0, count = c0 % GROUP // PACK, wc_raw[c0].shape[2] // PACK
-            copy(
-                out=wc_bf[:].rearrange("p (t m j) -> p m j t", t=PACK, j=PACK)[:, m0 : m0 + count],
-                in_=wc_raw[c0][:].rearrange("p j (m t) -> p m j t", t=PACK),
+        def weave_wc(g):
+            nc.scalar.copy(
+                out=wc_bf[g][:].rearrange("p (t m j) -> p m j t", t=PACK, j=PACK),
+                in_=wc_raw[g][:].rearrange("p j (m t) -> p m j t", t=PACK),
             )
 
-        def quantise_wc(g, wc_bf, tag):
-            wc_codes[g] = keep.tile([P, GROUP], U32, name="wc_codes%d" % g, tag=tag, align_bytes=64)
-            nc.vector.quantize_mx(out=wc_codes[g][:].bitcast(FP8X4), scales=wc_s[g][:], in_=wc_bf[:])
+        def quantise_wc(g):
+            nc.vector.quantize_mx(out=wc_w[g][:].bitcast(FP8X4), scales=wc_s[g][:], in_=wc_bf[g][:])
 
-        def add_pass(g, j0, n, t, term):
+        def add_pass(g, j0, t, term):
             done = passes.setdefault((g, j0, t), [])
             if not done:
                 sums[g, j0, t] = psum.tile([P, BANK], F32, name="acc")
             done.append(term)
-            own = slice(t * P, (t + 1) * P)
-            cols = slice(j0, j0 + n)
+            cols = slice(j0, j0 + BANK)
             if term == TOKEN:
-                at = j0 % BANK
-                w, w_scale = wc_codes[g][:, own], wc_s[g][:, own]
-                x, x_scale = v_w[j0 // BANK][:, at : at + n], v_s[:, cols]
+                own = slice(t * P, (t + 1) * P)
+                w, w_scale = wc_w[g][:, own], wc_s[g][:, own]
+                x, x_scale = v_w[j0][:], v_s[:, cols]
             else:
-                w, w_scale = uc_w[term][g][:, own], uc_s[SCALE_ROWS * term :, dealt(g, t)]
+                w, w_scale = uc_w[term][:, dealt(g, t)], uc_s[SCALE_ROWS * term :, dealt(g, t)]
                 x, x_scale = h_w[term][:, cols], h_s[term][:, cols]
             nc.tensor.matmul_mx(
-                out=sums[g, j0, t][:, :n],
+                out=sums[g, j0, t][:],
                 lhsT=w.bitcast(FP8X4),
                 lhsT_scale=w_scale,
                 rhs=x.bitcast(FP8X4),
@@ -205,26 +201,23 @@ def tile_list_gru_token_candidate_kernel(
                 stop=(len(done) == PASSES),
             )
 
-        def open_sums(g, j0, n, terms):
-            for term in terms:
-                for t in range(PACK):
-                    add_pass(g, j0, n, t, term)
+        def open_sums(g, j0, term):
+            for t in range(PACK):
+                add_pass(g, j0, t, term)
 
-        def y_planes(g, j0, n):
-            rows = y_rows[g, j0 // BANK][:].rearrange("p (t j) -> p t j", t=PACK)
-            return rows[:, :, j0 % BANK : j0 % BANK + n]
-
-        def make_y(g, j0, n, terms, scalar_gains):
-            if j0 % BANK == 0:
-                y_rows[g, j0 // BANK] = rows_tile("y%d_%d" % (g, j0), [P, PACK * BANK])
-            y = y_planes(g, j0, n)
-            rows = out_0[GROUP * g : GROUP * (g + 1), j0 : j0 + n].rearrange("(p t) j -> p t j", t=PACK)
+        def make_y(g, j0, terms, scalar_gains):
+            if y_rows:
+                y_rows[g, j0] = rows_tile("y%d_%d" % (g, j0))
+            else:
+                y_rows[g, j0] = kept("y_first", PACK * BANK, F32, "wc_raw1")
+            y = planes(y_rows[g, j0], 0, BANK)
+            rows = out_0[GROUP * g : GROUP * (g + 1), j0 : j0 + BANK].rearrange("(p t) j -> p t j", t=PACK)
             for pair in range(0, PACK, 2):
                 for t in (pair, pair + 1):
                     for term in terms:
-                        add_pass(g, j0, n, t, term)
+                        add_pass(g, j0, t, term)
                     nc.scalar.activation(
-                        out=y[:, t, :], in_=sums[g, j0, t][:, :n], func=ACT.Tanh, bias=bias[:, g, t : t + 1]
+                        out=y[:, t, :], in_=sums[g, j0, t][:], func=ACT.Tanh, bias=bias[:, g, t : t + 1]
                     )
                 for t in (pair, pair + 1):
                     row = y[:, t, :]
@@ -234,16 +227,21 @@ def tile_list_gru_token_candidate_kernel(
                         nc.vector.tensor_scalar(out=row, in0=row, scalar1=gains[:, g, t : t + 1], scalar2=None, op0=MULT)
                 nc.sync.dma_start(rows[:, pair : pair + 2, :], y[:, pair : pair + 2, :])
 
-        def quantise_y(g, j0, n, copy, y_bf=None):
-            if y_bf is None:
-                y_bf = ring.tile([P, PACK * BANK], BF16, name="y_bf", align_bytes=64, bufs=3)
-            weave(copy, y_bf[:, : PACK * n], y_planes(g, j0, n))
-            y_w = keep.tile([P, n], U32, name="y_w%d_%d" % (g, j0), align_bytes=64)
+        def weave_y(g, j0, c0, n, copy):
+            if (g, j0) not in y_bf:
+                y_bf[g, j0] = kept("y_bf%d_%d" % (g, j0), PACK * BANK, BF16, "gate0_%d" % len(y_bf))
+            weave(copy, y_bf[g, j0][:, PACK * c0 : PACK * (c0 + n)], planes(y_rows[g, j0], c0, n))
+
+        def quantise_y(g, j0):
+            cols = slice(j0, j0 + BANK)
             nc.vector.quantize_mx(
-                out=y_w[:].bitcast(FP8X4), scales=y_s[SCALE_ROWS * g :, j0 : j0 + n], in_=y_bf[:, : PACK * n]
+                out=y_w[g][:, cols].bitcast(FP8X4), scales=y_s[SCALE_ROWS * g :, cols], in_=y_bf[g, j0][:]
             )
+
+        def store_words(g, j0, n):
             nc.sync.dma_start(
-                out_1[g, :, j0 : j0 + n, :].rearrange("p m t -> p (m t)").bitcast(I32), y_w[:].bitcast(I32)
+                out_1[g, :, j0 : j0 + n, :].rearrange("p m t -> p (m t)").bitcast(I32),
+                y_w[g][:, j0 : j0 + n].bitcast(I32),
             )
 
         nc.vector.memset(tab_s[:].bitcast(I32), 0)
@@ -255,98 +253,87 @@ def tile_list_gru_token_candidate_kernel(
 
         nc.sync.dma_start(offsets[:], offs)
         nc.sync.dma_start(wr_raw[:].bitcast(I32), wr_words[0].bitcast(I32))
-        load_uc(0, 0)
         load_scale_rows(tab_s, tab_scales, 1)
         nc.sync.dma_start(tab_w[:], tab_words[0].rearrange("p t i -> p (t i)").bitcast(I32))
         load_scale_rows(wr_s_raw, wr_scales, 1)
-        for t in range(PACK):
+        for t in range(PACK - 1):
             load_state(0, t)
+        load_wc(0)
+        load_state(0, PACK - 1)
         load_state(1, 0)
         load_state(1, 1)
         load_scale_rows(uc_s_raw, uc_scales, GROUPS)
+        load_uc(0)
         load_state(1, 2)
-        load_wc(0, rows_tile("wc_raw0", [P, PACK, GROUP]))
-        load_wc(GROUP, keep.tile([P, PACK, SLICE], F32, name="wc_raw_third", align_bytes=64))
+        load_uc(1)
         load_state(1, 3)
-        load_uc(1, 0)
+        load_wc(1)
         nc.sync.dma_start(bias[:], b.rearrange("(g p t) -> p g t", p=P, t=PACK))
         nc.sync.dma_start(gains[:], gain.rearrange("(g p t) -> p g t", p=P, t=PACK))
-        load_uc(0, 1)
-        load_wc(GROUP + SLICE, keep.tile([P, PACK, SLICE], F32, name="wc_raw_last", tag="late_rows", align_bytes=64))
-        load_uc(1, 1)
 
-        nc.vector.tensor_copy(v_s[:], tab_s[:].indirect(offsets[:]))
         deal_narrow(wr_w[:].bitcast(U16), wr_raw[:].bitcast(U16), 2)
-        v_w[0] = keep.tile([P, BANK], U32, name="v_w0", align_bytes=64)
+        nc.vector.tensor_copy(v_s[:], tab_s[:].indirect(offsets[:]))
+        v_w[0] = kept("v_w0", BANK, U32)
         nc.vector.tensor_copy(v_w[0][:], tab_w[:].bitcast(U32).indirect(picks(0, BANK)))
         for a in range(GROUPS):
             deal_narrow(wr_s[a][:], wr_s_raw[:, GROUP * a : GROUP * (a + 1)], 1)
-        v_w[1] = keep.tile([P, BANK], U32, name="v_w1", tag="late_words", align_bytes=64)
-        nc.vector.tensor_copy(v_w[1][:], tab_w[:].bitcast(U32).indirect(picks(BANK, BANK)))
+        v_w[BANK] = kept("v_w1", BANK, U32, "late_words")
+        nc.vector.tensor_copy(v_w[BANK][:], tab_w[:].bitcast(U32).indirect(picks(BANK, BANK)))
 
         for a in range(GROUPS):
             for t in range(PACK):
-                make_gate(a, t, 0)
-                make_gate(a, t, BANK)
+                for j0 in (0, BANK):
+                    make_gate(a, t, j0)
 
         for t in range(PACK):
-            width = BANK if t in (0, PACK - 1) else S
+            width = BANK if t == 0 else S
             for j0 in range(0, S, width):
                 gather_state(0, t, j0, width)
-        quantise_h(0, 0, BANK, on_scalar)
-
-        h_rows[1, 0] = keep.tile([P, PACK * FIRST], F32, name="room_first", tag="room0", align_bytes=64)
-        gather_state(1, 0, 0, FIRST)
-        gather_state(1, 1, 0, FIRST)
-        quantise_h(0, BANK, BANK, on_scalar)
+        for t in range(PACK - 2):
+            gather_state(1, t, 0, S)
+        gather_state(1, 2, 0, BANK)
+        weave_wc(0)
+        wc_w[0] = kept("wc_w0", GROUP, U32, "gate1_0")
+        quantise_wc(0)
+        weave_h(0, 0, S, on_scalar)
+        h_w[0] = kept("h_w0", S, U32, "gate1_1")
+        quantise_h(0, 0, S)
         deal_narrow(uc_s[:], uc_s_raw[:], 1)
-        deal_uc(0, 0)
-        gather_state(1, 2, 0, FIRST)
-        early_wc = keep.tile([P, PACK * GROUP], BF16, name="early_wc", align_bytes=64)
-        late_wc = keep.tile([P, PACK * GROUP], BF16, name="late_wc", align_bytes=64)
-        weave_wc(0, on_scalar, early_wc)
-        weave_wc(GROUP, on_scalar, late_wc)
-        open_sums(0, 0, SLICE, (0,))
-        open_sums(0, BANK, BANK, (0,))
+        deal_uc(0)
+        deal_uc(1)
+        open_sums(0, 0, TOKEN)
+        for g in range(GROUPS):
+            open_sums(g, 0, 0)
 
         last = PACK - 1
-        gather_state(1, last, 0, SLICE)
-        first_bf = keep.tile([P, PACK * SLICE], BF16, name="first_bf", tag="room1", align_bytes=64)
-        quantise_h(1, 0, SLICE, on_scalar, first_bf)
-        deal_uc(1, 0)
-        gather_state(1, last, SLICE, SLICE)
-        quantise_wc(0, early_wc, "last_gate0")
-        open_sums(0, 0, SLICE, (TOKEN,))
-        second_bf = keep.tile([P, PACK * SLICE], BF16, name="second_bf", align_bytes=64)
-        quantise_h(1, SLICE, SLICE, on_scalar, second_bf)
-        make_y(0, 0, SLICE, (1,), PACK)
-        open_sums(0, BANK, BANK, (TOKEN,))
-        gather_state(1, last, BANK, FIRST - BANK)
-        third_bf = keep.tile([P, PACK * BANK], BF16, name="third_bf", tag="room1", align_bytes=64)
-        weave(on_vector, third_bf[:, : PACK * (FIRST - BANK)], h_planes(1, BANK, FIRST - BANK))
-        deal_uc(0, 1)
-        weave_wc(GROUP + SLICE, on_vector, late_wc)
-        deal_uc(1, 1)
-        quantise_wc(1, late_wc, "wc_codes1")
-        make_y(0, SLICE, SLICE, (0, TOKEN, 1), PACK)
-        h_rows[1, FIRST] = keep.tile([P, PACK * (S - FIRST)], F32, name="room_late", tag="late_rows", align_bytes=64)
-        for t in range(PACK):
-            gather_state(1, t, FIRST, S - FIRST)
-        weave(on_vector, third_bf[:, PACK * (FIRST - BANK) :], h_planes(1, FIRST, S - FIRST))
-        nc.vector.quantize_mx(out=h_w[1][:, BANK:].bitcast(FP8X4), scales=h_s[1][:, BANK:], in_=third_bf[:])
+        for step in (lambda j0: gather_state(1, last, j0, SLICE), lambda j0: weave_h(1, j0, SLICE, on_vector), lambda j0: quantise_h(1, j0, SLICE)):
+            for j0 in range(0, BANK, SLICE):
+                step(j0)
+        weave_wc(1)
+        quantise_wc(1)
+        gather_state(1, 2, BANK, BANK)
+        gather_state(1, last, BANK, BANK)
+        h_bf[1, BANK] = kept("late_bf", PACK * BANK, BF16, "wc_bf1")
+        weave_h(1, BANK, BANK, on_vector)
+        quantise_h(1, BANK, BANK)
 
-        make_y(1, 0, BANK, (0, TOKEN, 1), 0)
-        make_y(0, BANK, BANK, (1,), 0)
-        make_y(1, BANK, BANK, (0, TOKEN, 1), 0)
+        make_y(0, 0, (1,), PACK)
+        make_y(1, 0, (1, TOKEN), 0)
+        make_y(0, BANK, (0, TOKEN, 1), 0)
+        make_y(1, BANK, (0, TOKEN, 1), 0)
 
-        held_bf = keep.tile([P, PACK * BANK], BF16, name="held_bf", tag="late_rows", align_bytes=64)
-        quantise_y(1, 0, BANK, on_vector, held_bf)
-        next_bf = keep.tile([P, PACK * BANK], BF16, name="next_bf", tag="late_rows", align_bytes=64)
-        quantise_y(0, 0, BANK, on_vector, next_bf)
-        last_bf = keep.tile([P, PACK * BANK], BF16, name="last_bf", tag="after_tanh", align_bytes=64)
-        quantise_y(0, BANK, BANK, on_scalar, last_bf)
-        quantise_y(1, BANK, SLICE, on_vector)
-        quantise_y(1, BANK + SLICE, SLICE, on_scalar)
+        for g in range(GROUPS):
+            weave_y(g, 0, 0, BANK, on_vector)
+        for g in range(GROUPS):
+            quantise_y(g, 0)
+            store_words(g, 0, BANK)
+        weave_y(0, BANK, 0, BANK, on_vector)
+        quantise_y(0, BANK)
+        store_words(0, BANK, BANK)
+        weave_y(1, BANK, 0, SHARE, on_scalar)
+        weave_y(1, BANK, SHARE, BANK - SHARE, on_vector)
+        quantise_y(1, BANK)
+        store_words(1, BANK, BANK)
         for q in range(QUADS):
             nc.sync.dma_start(
                 out_2[:, SCALE_ROWS * q : SCALE_ROWS * (q + 1), :].bitcast(I32),

@@ -26,6 +26,7 @@ LINE = 16
 PAIR = 2
 BANK = 512
 SLICE = 256
+QUARTER = H // 4
 SHARE = 256
 TOKEN = GROUPS
 PASSES = GROUPS + 1
@@ -51,13 +52,15 @@ def tile_list_gru_token_candidate_kernel(
         tab_w = kept("tab_w", T, I32)
         wr_raw = kept("wr_raw", 2 * H, U8)
         wr_w = kept("wr_w", 2 * H, U8)
-        wr_s_raw = kept("wr_s_raw", H, U8, "late_words")
+        wr_s_raw = kept("wr_s_raw", H, U8)
         wr_s = [kept("wr_s%d" % a, GROUP, U8) for a in range(GROUPS)]
         uc_s_raw = kept("uc_s_raw", H, U8)
         uc_s = kept("uc_s", H, U8)
         uc_raw = [kept("uc_raw%d" % a, H, I32) for a in range(GROUPS)]
         uc_w = [kept("uc_w%d" % a, H, U32) for a in range(GROUPS)]
-        wc_raw = [keep.tile([P, PACK, GROUP], F32, name="wc_raw%d" % g, align_bytes=64) for g in range(GROUPS)]
+        wc_raw = {0: keep.tile([P, PACK, GROUP], F32, name="wc_raw0", align_bytes=64)}
+        for c0 in (GROUP, GROUP + QUARTER):
+            wc_raw[c0] = keep.tile([P, PACK, QUARTER], F32, name="wc_raw%d" % c0, align_bytes=64)
         wc_bf = [kept("wc_bf%d" % g, PACK * GROUP, BF16) for g in range(GROUPS)]
         wc_w = {1: kept("wc_w1", GROUP, U32)}
         wc_s = [kept("wc_s%d" % g, GROUP, U8) for g in range(GROUPS)]
@@ -96,14 +99,15 @@ def tile_list_gru_token_candidate_kernel(
             rows = gT[GROUP * a : GROUP * (a + 1), :].rearrange("(p t) w -> p t w", t=PACK)
             nc.sync.dma_start(state[a, t][:], rows[:, t, :])
 
-        def load_wc(g):
-            nc.sync.dma_start(wc_raw[g][:], wc[:, GROUP * g : GROUP * (g + 1)].rearrange("(p j) n -> p j n", j=PACK))
+        def load_wc(c0):
+            cols = slice(c0, c0 + wc_raw[c0].shape[2])
+            nc.sync.dma_start(wc_raw[c0][:], wc[:, cols].rearrange("(p j) n -> p j n", j=PACK))
 
         def load_uc(a):
             nc.sync.dma_start(uc_raw[a][:], uc_words[a].rearrange("p e i -> p (e i)").bitcast(I32))
 
-        def deal_narrow(dst, src, size):
-            nc.vector.tensor_copy(
+        def deal_narrow(dst, src, size, copy=on_vector):
+            copy(
                 out=dst.rearrange("p (t c i) -> p c t i", t=PACK, i=LINE // size),
                 in_=src.rearrange("p (c i t) -> p c t i", t=PACK, i=LINE // size),
             )
@@ -169,10 +173,11 @@ def tile_list_gru_token_candidate_kernel(
                 in_=woven_h(a, j0, n),
             )
 
-        def weave_wc(g):
+        def weave_wc(c0):
+            m0, count = c0 % GROUP // PACK, wc_raw[c0].shape[2] // PACK
             nc.scalar.copy(
-                out=wc_bf[g][:].rearrange("p (t m j) -> p m j t", t=PACK, j=PACK),
-                in_=wc_raw[g][:].rearrange("p j (m t) -> p m j t", t=PACK),
+                out=wc_bf[c0 // GROUP][:].rearrange("p (t m j) -> p m j t", t=PACK, j=PACK)[:, m0 : m0 + count],
+                in_=wc_raw[c0][:].rearrange("p j (m t) -> p m j t", t=PACK),
             )
 
         def quantise_wc(g):
@@ -209,7 +214,7 @@ def tile_list_gru_token_candidate_kernel(
             if y_rows:
                 y_rows[g, j0] = rows_tile("y%d_%d" % (g, j0))
             else:
-                y_rows[g, j0] = kept("y_first", PACK * BANK, F32, "wc_raw1")
+                y_rows[g, j0] = kept("y_first", PACK * BANK, F32, "wc_raw768")
             y = planes(y_rows[g, j0], 0, BANK)
             rows = out_0[GROUP * g : GROUP * (g + 1), j0 : j0 + BANK].rearrange("(p t) j -> p t j", t=PACK)
             for pair in range(0, PACK, 2):
@@ -258,16 +263,17 @@ def tile_list_gru_token_candidate_kernel(
         load_scale_rows(wr_s_raw, wr_scales, 1)
         for t in range(PACK - 1):
             load_state(0, t)
-        load_wc(0)
+        load_uc(0)
         load_state(0, PACK - 1)
         load_state(1, 0)
         load_state(1, 1)
         load_scale_rows(uc_s_raw, uc_scales, GROUPS)
-        load_uc(0)
+        load_wc(0)
         load_state(1, 2)
-        load_uc(1)
         load_state(1, 3)
-        load_wc(1)
+        load_uc(1)
+        load_wc(GROUP)
+        load_wc(GROUP + QUARTER)
         nc.sync.dma_start(bias[:], b.rearrange("(g p t) -> p g t", p=P, t=PACK))
         nc.sync.dma_start(gains[:], gain.rearrange("(g p t) -> p g t", p=P, t=PACK))
 
@@ -276,8 +282,8 @@ def tile_list_gru_token_candidate_kernel(
         v_w[0] = kept("v_w0", BANK, U32)
         nc.vector.tensor_copy(v_w[0][:], tab_w[:].bitcast(U32).indirect(picks(0, BANK)))
         for a in range(GROUPS):
-            deal_narrow(wr_s[a][:], wr_s_raw[:, GROUP * a : GROUP * (a + 1)], 1)
-        v_w[BANK] = kept("v_w1", BANK, U32, "late_words")
+            deal_narrow(wr_s[a][:], wr_s_raw[:, GROUP * a : GROUP * (a + 1)], 1, nc.gpsimd.tensor_copy)
+        v_w[BANK] = kept("v_w1", BANK, U32)
         nc.vector.tensor_copy(v_w[BANK][:], tab_w[:].bitcast(U32).indirect(picks(BANK, BANK)))
 
         for a in range(GROUPS):
@@ -289,30 +295,31 @@ def tile_list_gru_token_candidate_kernel(
             width = BANK if t == 0 else S
             for j0 in range(0, S, width):
                 gather_state(0, t, j0, width)
-        for t in range(PACK - 2):
+        for t in (0, 1):
             gather_state(1, t, 0, S)
         gather_state(1, 2, 0, BANK)
-        weave_wc(0)
-        wc_w[0] = kept("wc_w0", GROUP, U32, "gate1_0")
-        quantise_wc(0)
+        deal_uc(0)
         weave_h(0, 0, S, on_scalar)
+        deal_narrow(uc_s[:], uc_s_raw[:], 1)
         h_w[0] = kept("h_w0", S, U32, "gate1_1")
         quantise_h(0, 0, S)
-        deal_narrow(uc_s[:], uc_s_raw[:], 1)
-        deal_uc(0)
+        weave_wc(0)
+        wc_w[0] = kept("wc_w0", GROUP, U32, "gate1_2_0")
+        quantise_wc(0)
         deal_uc(1)
+        open_sums(0, 0, 0)
         open_sums(0, 0, TOKEN)
-        for g in range(GROUPS):
-            open_sums(g, 0, 0)
+        open_sums(1, 0, 0)
 
         last = PACK - 1
         for step in (lambda j0: gather_state(1, last, j0, SLICE), lambda j0: weave_h(1, j0, SLICE, on_vector), lambda j0: quantise_h(1, j0, SLICE)):
             for j0 in range(0, BANK, SLICE):
                 step(j0)
-        weave_wc(1)
+        weave_wc(GROUP)
+        weave_wc(GROUP + QUARTER)
         quantise_wc(1)
-        gather_state(1, 2, BANK, BANK)
-        gather_state(1, last, BANK, BANK)
+        for t in (last, 2):
+            gather_state(1, t, BANK, BANK)
         h_bf[1, BANK] = kept("late_bf", PACK * BANK, BF16, "wc_bf1")
         weave_h(1, BANK, BANK, on_vector)
         quantise_h(1, BANK, BANK)

@@ -27,7 +27,6 @@ PAIR = 2
 BANK = 512
 SLICE = 256
 QUARTER = H // 4
-SHARE = 256
 TOKEN = GROUPS
 PASSES = GROUPS + 1
 
@@ -160,7 +159,7 @@ def tile_list_gru_token_candidate_kernel(
             )
 
         def woven_h(a, j0, n):
-            first = j0 // BANK * BANK if a else 0
+            first = max(j for group, j in h_bf if group == a and j <= j0)
             return h_bf[a, first][:, PACK * (j0 - first) : PACK * (j0 - first + n)]
 
         def weave_h(a, j0, n, copy):
@@ -210,31 +209,31 @@ def tile_list_gru_token_candidate_kernel(
             for t in range(PACK):
                 add_pass(g, j0, t, term)
 
-        def make_y(g, j0, terms, scalar_gains):
-            if y_rows:
-                y_rows[g, j0] = rows_tile("y%d_%d" % (g, j0))
-            else:
-                y_rows[g, j0] = kept("y_first", PACK * BANK, F32, "wc_raw768")
+        def make_y(g, j0, terms, scalar_gains, second_pair=None):
+            y_rows[g, j0] = rows_tile("y%d_%d" % (g, j0))
             y = planes(y_rows[g, j0], 0, BANK)
             rows = out_0[GROUP * g : GROUP * (g + 1), j0 : j0 + BANK].rearrange("(p t) j -> p t j", t=PACK)
+            tanh = [y[:, t, :] for t in range(PACK)]
+            if second_pair is not None:
+                tanh[2:] = [second_pair[:, :BANK], second_pair[:, BANK:]]
             for pair in range(0, PACK, 2):
                 for t in (pair, pair + 1):
                     for term in terms:
                         add_pass(g, j0, t, term)
                     nc.scalar.activation(
-                        out=y[:, t, :], in_=sums[g, j0, t][:], func=ACT.Tanh, bias=bias[:, g, t : t + 1]
+                        out=tanh[t], in_=sums[g, j0, t][:], func=ACT.Tanh, bias=bias[:, g, t : t + 1]
                     )
                 for t in (pair, pair + 1):
                     row = y[:, t, :]
                     if t < scalar_gains:
                         nc.scalar.activation(out=row, in_=row, func=ACT.Copy, scale=gains[:, g, t : t + 1])
                     else:
-                        nc.vector.tensor_scalar(out=row, in0=row, scalar1=gains[:, g, t : t + 1], scalar2=None, op0=MULT)
+                        nc.vector.tensor_scalar(out=row, in0=tanh[t], scalar1=gains[:, g, t : t + 1], scalar2=None, op0=MULT)
                 nc.sync.dma_start(rows[:, pair : pair + 2, :], y[:, pair : pair + 2, :])
 
         def weave_y(g, j0, c0, n, copy):
             if (g, j0) not in y_bf:
-                y_bf[g, j0] = kept("y_bf%d_%d" % (g, j0), PACK * BANK, BF16, "gate0_%d" % len(y_bf))
+                y_bf[g, j0] = kept("y_bf%d_%d" % (g, j0), PACK * BANK, BF16, ("wc_raw512", "wc_bf0", "gate0_0", "gate0_1")[len(y_bf)])
             weave(copy, y_bf[g, j0][:, PACK * c0 : PACK * (c0 + n)], planes(y_rows[g, j0], c0, n))
 
         def quantise_y(g, j0):
@@ -251,7 +250,7 @@ def tile_list_gru_token_candidate_kernel(
 
         nc.vector.memset(tab_s[:].bitcast(I32), 0)
         nc.vector.memset(wr_s_raw[:].bitcast(I32), 0)
-        nc.gpsimd.memset(uc_s_raw[:].bitcast(I32), 0)
+        nc.vector.memset(uc_s_raw[:].bitcast(I32), 0)
         warm = keep.tile([P, 2], F32, name="warm")
         nc.vector.memset(warm[:], 0.0)
         nc.scalar.activation(out=warm[:, 1:2], in_=warm[:, 0:1], func=ACT.Sigmoid)
@@ -320,13 +319,15 @@ def tile_list_gru_token_candidate_kernel(
         quantise_wc(1)
         for t in (last, 2):
             gather_state(1, t, BANK, BANK)
-        h_bf[1, BANK] = kept("late_bf", PACK * BANK, BF16, "wc_bf1")
-        weave_h(1, BANK, BANK, on_vector)
-        quantise_h(1, BANK, BANK)
-
-        make_y(0, 0, (1,), PACK)
-        make_y(1, 0, (1, TOKEN), 0)
-        make_y(0, BANK, (0, TOKEN, 1), 0)
+        h_bf[1, BANK] = kept("late_bf", PACK * SLICE, BF16, "wc_bf1")
+        weave_h(1, BANK, SLICE, on_vector)
+        make_y(0, 0, (1,), 2, kept("first_tanh", 2 * BANK, F32, "wc_raw768"))
+        h_bf[1, S - SLICE] = kept("last_bf", PACK * SLICE, BF16, "wc_raw768")
+        weave_h(1, S - SLICE, SLICE, on_vector)
+        for j0 in (BANK, S - SLICE):
+            quantise_h(1, j0, SLICE)
+        make_y(1, 0, (1, TOKEN), 0, kept("second_tanh", 2 * BANK, F32, "wc_raw512"))
+        make_y(0, BANK, (0, TOKEN, 1), 0, kept("third_tanh", 2 * BANK, F32, "wc_bf0"))
         make_y(1, BANK, (0, TOKEN, 1), 0)
 
         for g in range(GROUPS):
@@ -334,13 +335,11 @@ def tile_list_gru_token_candidate_kernel(
         for g in range(GROUPS):
             quantise_y(g, 0)
             store_words(g, 0, BANK)
-        weave_y(0, BANK, 0, BANK, on_vector)
-        quantise_y(0, BANK)
-        store_words(0, BANK, BANK)
-        weave_y(1, BANK, 0, SHARE, on_scalar)
-        weave_y(1, BANK, SHARE, BANK - SHARE, on_vector)
-        quantise_y(1, BANK)
-        store_words(1, BANK, BANK)
+        weave_y(0, BANK, 0, BANK, on_scalar)
+        weave_y(1, BANK, 0, BANK, on_vector)
+        for g in range(GROUPS):
+            quantise_y(g, BANK)
+            store_words(g, BANK, BANK)
         for q in range(QUADS):
             nc.sync.dma_start(
                 out_2[:, SCALE_ROWS * q : SCALE_ROWS * (q + 1), :].bitcast(I32),

@@ -27,6 +27,7 @@ PAIR = 2
 BANK = 512
 SLICE = 256
 QUARTER = H // 4
+SHARE = 128
 TOKEN = GROUPS
 PASSES = GROUPS + 1
 
@@ -319,13 +320,10 @@ def tile_list_gru_token_candidate_kernel(
         quantise_wc(1)
         for t in (last, 2):
             gather_state(1, t, BANK, BANK)
-        h_bf[1, BANK] = kept("late_bf", PACK * SLICE, BF16, "wc_bf1")
-        weave_h(1, BANK, SLICE, on_vector)
-        make_y(0, 0, (1,), 2, kept("first_tanh", 2 * BANK, F32, "wc_raw768"))
-        h_bf[1, S - SLICE] = kept("last_bf", PACK * SLICE, BF16, "wc_raw768")
-        weave_h(1, S - SLICE, SLICE, on_vector)
-        for j0 in (BANK, S - SLICE):
-            quantise_h(1, j0, SLICE)
+        h_bf[1, BANK] = kept("late_bf", PACK * BANK, BF16, "wc_bf1")
+        weave_h(1, BANK, BANK, on_vector)
+        quantise_h(1, BANK, BANK)
+        make_y(0, 0, (1,), 2)
         make_y(1, 0, (1, TOKEN), 0, kept("second_tanh", 2 * BANK, F32, "wc_raw512"))
         make_y(0, BANK, (0, TOKEN, 1), 0, kept("third_tanh", 2 * BANK, F32, "wc_bf0"))
         make_y(1, BANK, (0, TOKEN, 1), 0)
@@ -336,7 +334,8 @@ def tile_list_gru_token_candidate_kernel(
             quantise_y(g, 0)
             store_words(g, 0, BANK)
         weave_y(0, BANK, 0, BANK, on_scalar)
-        weave_y(1, BANK, 0, BANK, on_vector)
+        weave_y(1, BANK, 0, SHARE, on_scalar)
+        weave_y(1, BANK, SHARE, BANK - SHARE, on_vector)
         for g in range(GROUPS):
             quantise_y(g, BANK)
             store_words(g, BANK, BANK)

@@ -27,6 +27,7 @@ PAIR = 2
 BANK = 512
 SLICE = 256
 QUARTER = H // 4
+FIRST = 768
 SHARE = 128
 TOKEN = GROUPS
 PASSES = GROUPS + 1
@@ -69,11 +70,11 @@ def tile_list_gru_token_candidate_kernel(
         v_w = {}
         v_s = kept("v_s", S, U8)
         gate = {(a, t, 0): kept("gate%d_%d" % (a, t), S, F32) for a in range(GROUPS) for t in range(PACK - 2 * a)}
-        for piece in ((1, 2, 0), (1, 2, BANK), (1, 3, BANK)):
-            gate[piece] = kept("gate%d_%d_%d" % piece, BANK, F32)
+        for t, j0, n in ((2, 0, FIRST), (2, FIRST, S - FIRST), (3, 0, SLICE), (3, BANK, BANK)):
+            gate[1, t, j0] = kept("gate1_%d_%d" % (t, j0), n, F32)
         h_rows = [kept("h_rows%d" % a, PACK * S, F32) for a in range(GROUPS)]
-        gate[1, 3, 0] = h_rows[1][:, 2 * S + BANK : 3 * S]
-        h_bf = {(0, 0): kept("h_bf0", PACK * S, BF16), (1, 0): kept("h_bf1", PACK * BANK, BF16)}
+        gate[1, 3, SLICE] = h_rows[1][:, 2 * S + FIRST : 3 * S]
+        h_bf = {(0, 0): kept("h_bf0", PACK * S, BF16)}
         h_w = {1: kept("h_w1", S, U32)}
         h_s = [kept("h_s%d" % a, S, U8) for a in range(GROUPS)]
         y_w = [kept("y_w%d" % g, S, U32) for g in range(GROUPS)]
@@ -128,7 +129,7 @@ def tile_list_gru_token_candidate_kernel(
             return rows[:].rearrange("p (t w) -> p t w", t=PACK)[:, :, j0 : j0 + n]
 
         def gates(a, t, j0, n):
-            first = j0 // BANK * BANK if (a, t) >= (1, 2) else 0
+            first = max(j for group, plane, j in gate if (group, plane) == (a, t) and j <= j0)
             return gate[a, t, first][:, j0 - first : j0 - first + n]
 
         def make_gate(a, t, j0):
@@ -143,7 +144,9 @@ def tile_list_gru_token_candidate_kernel(
                 start=True,
                 stop=True,
             )
-            nc.scalar.activation(out=gates(a, t, j0, BANK), in_=acc[:], func=ACT.Sigmoid)
+            cuts = [j0] + [j for group, plane, j in sorted(gate) if (group, plane) == (a, t) and j0 < j < j0 + BANK]
+            for c0, c1 in zip(cuts, cuts[1:] + [j0 + BANK]):
+                nc.scalar.activation(out=gates(a, t, c0, c1 - c0), in_=acc[:, c0 - j0 : c1 - j0], func=ACT.Sigmoid)
 
         def gather_state(a, t, j0, n):
             nc.vector.tensor_tensor(
@@ -153,18 +156,18 @@ def tile_list_gru_token_candidate_kernel(
                 MULT,
             )
 
-        def weave(copy, woven, planar):
+        def weave(copy, woven, planar, some=slice(0, PACK)):
             copy(
-                out=woven.rearrange("p (c i t) -> p c t i", t=PACK, i=PAIR),
-                in_=planar.rearrange("p t (c i) -> p c t i", i=PAIR),
+                out=woven.rearrange("p (c i t) -> p c t i", t=PACK, i=PAIR)[:, :, some, :],
+                in_=planar.rearrange("p t (c i) -> p c t i", i=PAIR)[:, :, some, :],
             )
 
         def woven_h(a, j0, n):
             first = max(j for group, j in h_bf if group == a and j <= j0)
             return h_bf[a, first][:, PACK * (j0 - first) : PACK * (j0 - first + n)]
 
-        def weave_h(a, j0, n, copy):
-            weave(copy, woven_h(a, j0, n), planes(h_rows[a], j0, n))
+        def weave_h(a, j0, n, copy, some=slice(0, PACK)):
+            weave(copy, woven_h(a, j0, n), planes(h_rows[a], j0, n), some)
 
         def quantise_h(a, j0, n):
             nc.vector.quantize_mx(
@@ -297,7 +300,7 @@ def tile_list_gru_token_candidate_kernel(
                 gather_state(0, t, j0, width)
         for t in (0, 1):
             gather_state(1, t, 0, S)
-        gather_state(1, 2, 0, BANK)
+        gather_state(1, 2, 0, FIRST)
         deal_uc(0)
         weave_h(0, 0, S, on_scalar)
         deal_narrow(uc_s[:], uc_s_raw[:], 1)
@@ -306,20 +309,22 @@ def tile_list_gru_token_candidate_kernel(
         weave_wc(0)
         wc_w[0] = kept("wc_w0", GROUP, U32, "gate1_2_0")
         quantise_wc(0)
+        h_bf[1, 0] = kept("h_bf1", PACK * BANK, BF16, "wc_raw0")
+        weave_h(1, 0, BANK, on_scalar, slice(0, 2))
         deal_uc(1)
         open_sums(0, 0, 0)
         open_sums(0, 0, TOKEN)
         open_sums(1, 0, 0)
 
         last = PACK - 1
-        for step in (lambda j0: gather_state(1, last, j0, SLICE), lambda j0: weave_h(1, j0, SLICE, on_vector), lambda j0: quantise_h(1, j0, SLICE)):
+        for step in (lambda j0: gather_state(1, last, j0, SLICE), lambda j0: weave_h(1, j0, SLICE, on_vector, slice(2, PACK)), lambda j0: quantise_h(1, j0, SLICE)):
             for j0 in range(0, BANK, SLICE):
                 step(j0)
         weave_wc(GROUP)
         weave_wc(GROUP + QUARTER)
         quantise_wc(1)
-        for t in (last, 2):
-            gather_state(1, t, BANK, BANK)
+        gather_state(1, last, BANK, BANK)
+        gather_state(1, 2, FIRST, S - FIRST)
         h_bf[1, BANK] = kept("late_bf", PACK * BANK, BF16, "wc_bf1")
         weave_h(1, BANK, BANK, on_vector)
         quantise_h(1, BANK, BANK)

@@ -69,8 +69,16 @@ def tile_list_gru_token_candidate_kernel(
         gains = keep.tile([P, GROUPS, PACK], F32, name="gains", align_bytes=64)
         v_w = {}
         v_s = kept("v_s", S, U8)
-        gate = {(a, t, 0): kept("gate%d_%d" % (a, t), S, F32) for a in range(GROUPS) for t in range(PACK - 2 * a)}
-        for t, j0, n in ((2, 0, FIRST), (2, FIRST, S - FIRST), (3, 0, SLICE), (3, BANK, BANK)):
+        gate = {(a, t, 0): kept("gate%d_%d" % (a, t), S, F32) for a in range(GROUPS) for t in range(PACK - 3 * a)}
+        for t, j0, n in (
+            (1, 0, BANK),
+            (1, BANK, BANK),
+            (2, 0, BANK),
+            (2, BANK, FIRST - BANK),
+            (2, FIRST, S - FIRST),
+            (3, 0, SLICE),
+            (3, BANK, BANK),
+        ):
             gate[1, t, j0] = kept("gate1_%d_%d" % (t, j0), n, F32)
         h_rows = [kept("h_rows%d" % a, PACK * S, F32) for a in range(GROUPS)]
         gate[1, 3, SLICE] = h_rows[1][:, 2 * S + FIRST : 3 * S]
@@ -213,13 +221,13 @@ def tile_list_gru_token_candidate_kernel(
             for t in range(PACK):
                 add_pass(g, j0, t, term)
 
-        def make_y(g, j0, terms, scalar_gains, second_pair=None):
+        def make_y(g, j0, terms, scalar_gains, apart=None):
             y_rows[g, j0] = rows_tile("y%d_%d" % (g, j0))
             y = planes(y_rows[g, j0], 0, BANK)
             rows = out_0[GROUP * g : GROUP * (g + 1), j0 : j0 + BANK].rearrange("(p t) j -> p t j", t=PACK)
             tanh = [y[:, t, :] for t in range(PACK)]
-            if second_pair is not None:
-                tanh[2:] = [second_pair[:, :BANK], second_pair[:, BANK:]]
+            if apart is not None:
+                tanh[PACK - 2] = apart[:]
             for pair in range(0, PACK, 2):
                 for t in (pair, pair + 1):
                     for term in terms:
@@ -298,13 +306,14 @@ def tile_list_gru_token_candidate_kernel(
             width = BANK if t == 0 else S
             for j0 in range(0, S, width):
                 gather_state(0, t, j0, width)
-        for t in (0, 1):
-            gather_state(1, t, 0, S)
-        gather_state(1, 2, 0, FIRST)
+        gather_state(1, 0, 0, S)
+        for t, end in ((1, S), (2, FIRST)):
+            gather_state(1, t, 0, BANK)
+            gather_state(1, t, BANK, end - BANK)
         deal_uc(0)
         weave_h(0, 0, S, on_scalar)
         deal_narrow(uc_s[:], uc_s_raw[:], 1)
-        h_w[0] = kept("h_w0", S, U32, "gate1_1")
+        h_w[0] = kept("h_w0", S, U32, "gate1_1_0")
         quantise_h(0, 0, S)
         weave_wc(0)
         wc_w[0] = kept("wc_w0", GROUP, U32, "gate1_2_0")
@@ -329,8 +338,8 @@ def tile_list_gru_token_candidate_kernel(
         weave_h(1, BANK, BANK, on_vector)
         quantise_h(1, BANK, BANK)
         make_y(0, 0, (1,), 2)
-        make_y(1, 0, (1, TOKEN), 0, kept("second_tanh", 2 * BANK, F32, "wc_raw512"))
-        make_y(0, BANK, (0, TOKEN, 1), 0, kept("third_tanh", 2 * BANK, F32, "wc_bf0"))
+        make_y(1, 0, (1, TOKEN), 0, kept("second_tanh", BANK, F32, "wc_raw512"))
+        make_y(0, BANK, (0, TOKEN, 1), 0, kept("third_tanh", BANK, F32, "wc_bf0"))
         make_y(1, BANK, (0, TOKEN, 1), 0)
 
         for g in range(GROUPS):

@@ -191,8 +191,10 @@ def tile_list_gru_token_candidate_kernel(
                 in_=wc_raw[c0][:].rearrange("p j (m t) -> p m j t", t=PACK),
             )
 
-        def quantise_wc(g):
-            nc.vector.quantize_mx(out=wc_w[g][:].bitcast(FP8X4), scales=wc_s[g][:], in_=wc_bf[g][:])
+        def quantise_wc(g, c0, n):
+            cols = slice(c0, c0 + n)
+            woven = wc_bf[g][:, PACK * c0 : PACK * (c0 + n)]
+            nc.vector.quantize_mx(out=wc_w[g][:, cols].bitcast(FP8X4), scales=wc_s[g][:, cols], in_=woven)
 
         def add_pass(g, j0, t, term):
             done = passes.setdefault((g, j0, t), [])
@@ -317,7 +319,7 @@ def tile_list_gru_token_candidate_kernel(
         quantise_h(0, 0, S)
         weave_wc(0)
         wc_w[0] = kept("wc_w0", GROUP, U32, "gate1_2_0")
-        quantise_wc(0)
+        quantise_wc(0, 0, GROUP)
         h_bf[1, 0] = kept("h_bf1", PACK * BANK, BF16, "wc_raw0")
         weave_h(1, 0, BANK, on_scalar, slice(0, 2))
         deal_uc(1)
@@ -331,12 +333,15 @@ def tile_list_gru_token_candidate_kernel(
                 step(j0)
         weave_wc(GROUP)
         weave_wc(GROUP + QUARTER)
-        quantise_wc(1)
+        for c0 in (0, QUARTER):
+            quantise_wc(1, c0, QUARTER)
         gather_state(1, last, BANK, BANK)
         gather_state(1, 2, FIRST, S - FIRST)
-        h_bf[1, BANK] = kept("late_bf", PACK * BANK, BF16, "wc_bf1")
-        weave_h(1, BANK, BANK, on_vector)
-        quantise_h(1, BANK, BANK)
+        h_bf[1, BANK] = wc_bf[1]
+        for j0 in (BANK, BANK + SLICE):
+            weave_h(1, j0, SLICE, on_vector)
+        for j0 in (BANK, BANK + SLICE):
+            quantise_h(1, j0, SLICE)
         make_y(0, 0, (1,), 2)
         make_y(1, 0, (1, TOKEN), 0, kept("second_tanh", BANK, F32, "wc_raw512"))
         make_y(0, BANK, (0, TOKEN, 1), 0, kept("third_tanh", BANK, F32, "wc_bf0"))

@@ -28,7 +28,7 @@ BANK = 512
 SLICE = 256
 QUARTER = H // 4
 FIRST = 768
-SHARE = 128
+SHARE = 256
 TOKEN = GROUPS
 PASSES = GROUPS + 1
 
@@ -223,13 +223,13 @@ def tile_list_gru_token_candidate_kernel(
             for t in range(PACK):
                 add_pass(g, j0, t, term)
 
-        def make_y(g, j0, terms, scalar_gains, apart=None):
+        def make_y(g, j0, terms, scalar_gains, apart=None, plane=PACK - 2):
             y_rows[g, j0] = rows_tile("y%d_%d" % (g, j0))
             y = planes(y_rows[g, j0], 0, BANK)
             rows = out_0[GROUP * g : GROUP * (g + 1), j0 : j0 + BANK].rearrange("(p t) j -> p t j", t=PACK)
             tanh = [y[:, t, :] for t in range(PACK)]
             if apart is not None:
-                tanh[PACK - 2] = apart[:]
+                tanh[plane] = apart
             for pair in range(0, PACK, 2):
                 for t in (pair, pair + 1):
                     for term in terms:
@@ -343,16 +343,21 @@ def tile_list_gru_token_candidate_kernel(
         for j0 in (BANK, BANK + SLICE):
             quantise_h(1, j0, SLICE)
         make_y(0, 0, (1,), 2)
-        make_y(1, 0, (1, TOKEN), 0, kept("second_tanh", BANK, F32, "wc_raw512"))
-        make_y(0, BANK, (0, TOKEN, 1), 0, kept("third_tanh", BANK, F32, "wc_bf0"))
+        y_bf[0, 0] = kept("y_bf0_0", PACK * BANK, BF16, "gate0_2")
+        weave_y(0, 0, 0, SLICE, on_vector)
+        make_y(1, 0, (1, TOKEN), 0, y_bf[0, 0][:, PACK * SLICE :].bitcast(F32), 1)
+        weave_y(0, 0, SLICE, SLICE, on_vector)
+        y_bf[1, 0] = kept("y_bf1_0", PACK * BANK, BF16, "wc_bf0")
+        weave_y(1, 0, 0, SLICE, on_vector)
+        make_y(0, BANK, (0, TOKEN, 1), 0, y_bf[1, 0][:, PACK * SLICE :].bitcast(F32), 1)
         make_y(1, BANK, (0, TOKEN, 1), 0)
 
-        for g in range(GROUPS):
-            weave_y(g, 0, 0, BANK, on_vector)
+        weave_y(1, 0, SLICE, SLICE, on_vector)
         for g in range(GROUPS):
             quantise_y(g, 0)
             store_words(g, 0, BANK)
-        weave_y(0, BANK, 0, BANK, on_scalar)
+        weave_y(0, BANK, 0, SLICE, on_vector)
+        weave_y(0, BANK, SLICE, SLICE, on_scalar)
         weave_y(1, BANK, 0, SHARE, on_scalar)
         weave_y(1, BANK, SHARE, BANK - SHARE, on_vector)
         for g in range(GROUPS):

@@ -364,7 +364,7 @@ def tile_list_gru_token_candidate_kernel(
             quantise_y(g, BANK)
             store_words(g, BANK, BANK)
         for q in range(QUADS):
-            nc.sync.dma_start(
+            nc.scalar.dma_start(
                 out_2[:, SCALE_ROWS * q : SCALE_ROWS * (q + 1), :].bitcast(I32),
                 y_s[32 * q : 32 * q + SCALE_ROWS * GROUPS, :].bitcast(I32),
             )

from contextlib import ExitStack

import concourse.mybir as mybir

K, H, T, S = 512, 1024, 2048, 1024
FLOPS = 2 * S * H * (2 * K + H)

F32 = mybir.dt.float32
BF16 = mybir.dt.bfloat16
I32 = mybir.dt.int32
U32 = mybir.dt.uint32
U16 = mybir.dt.uint16
U8 = mybir.dt.uint8
FP8X4 = mybir.dt.float8_e4m3fn_x4
FP4X4 = mybir.dt.float4_e2m1fn_x4
ACT = mybir.ActivationFunctionType
MULT = mybir.AluOpType.mult

P = 128
PACK = 4
GROUP = P * PACK
GROUPS = H // GROUP
QUADS = 4
SCALE_ROWS = 4
LINE = 16
PAIR = 2
BANK = 512
SLICE = 256
QUARTER = H // 4
FIRST = 768
SHARE = 256
TOKEN = GROUPS
PASSES = GROUPS + 1


def tile_list_gru_token_candidate_kernel(
    tc, tab_words, tab_scales, offs, gT, wr_words, wr_scales, wc, uc_words, uc_scales, b, gain, out_0, out_1, out_2
):
    nc = tc.nc
    with ExitStack() as ctx:
        keep = ctx.enter_context(tc.tile_pool(name="keep", bufs=1))
        ring = ctx.enter_context(tc.tile_pool(name="ring", bufs=2))
        psum = ctx.enter_context(tc.psum_pool(name="psum", bufs=8))

        def kept(name, width, dtype, tag=""):
            return keep.tile([P, width], dtype, name=name, tag=tag, align_bytes=64)

        def rows_tile(name):
            return ring.tile([P, T], F32, name=name, tag="rows", bufs=GROUPS * PACK)

        offsets = keep.tile([P, S // 16], U16, name="offsets")
        tab_s = kept("tab_s", T, U8)
        tab_w = kept("tab_w", T, I32)
        wr_raw = kept("wr_raw", 2 * H, U8)
        wr_w = kept("wr_w", 2 * H, U8)
        wr_s_raw = kept("wr_s_raw", H, U8)
        wr_s = [kept("wr_s%d" % a, GROUP, U8) for a in range(GROUPS)]
        uc_s_raw = kept("uc_s_raw", H, U8)
        uc_s = kept("uc_s", H, U8)
        uc_raw = [kept("uc_raw%d" % a, H, I32) for a in range(GROUPS)]
        uc_w = [kept("uc_w%d" % a, H, U32) for a in range(GROUPS)]
        wc_raw = {0: keep.tile([P, PACK, GROUP], F32, name="wc_raw0", align_bytes=64)}
        for c0 in (GROUP, GROUP + QUARTER):
            wc_raw[c0] = keep.tile([P, PACK, QUARTER], F32, name="wc_raw%d" % c0, align_bytes=64)
        wc_bf = [kept("wc_bf%d" % g, PACK * GROUP, BF16) for g in range(GROUPS)]
        wc_w = {1: kept("wc_w1", GROUP, U32)}
        wc_s = [kept("wc_s%d" % g, GROUP, U8) for g in range(GROUPS)]
        bias = keep.tile([P, GROUPS, PACK], F32, name="bias", align_bytes=64)
        gains = keep.tile([P, GROUPS, PACK], F32, name="gains", align_bytes=64)
        v_w = {}
        v_s = kept("v_s", S, U8)
        gate = {(a, t, 0): kept("gate%d_%d" % (a, t), S, F32) for a in range(GROUPS) for t in range(PACK - 3 * a)}
        for t, j0, n in (
            (1, 0, BANK),
            (1, BANK, BANK),
            (2, 0, BANK),
            (2, BANK, FIRST - BANK),
            (2, FIRST, S - FIRST),
            (3, 0, SLICE),
            (3, BANK, BANK),
        ):
            gate[1, t, j0] = kept("gate1_%d_%d" % (t, j0), n, F32)
        h_rows = [kept("h_rows%d" % a, PACK * S, F32) for a in range(GROUPS)]
        gate[1, 3, SLICE] = h_rows[1][:, 2 * S + FIRST : 3 * S]
        h_bf = {(0, 0): kept("h_bf0", PACK * S, BF16)}
        h_w = {1: kept("h_w1", S, U32)}
        h_s = [kept("h_s%d" % a, S, U8) for a in range(GROUPS)]
        y_w = [kept("y_w%d" % g, S, U32) for g in range(GROUPS)]
        y_s = kept("y_s", S, U8)
        state = {}
        y_rows = {}
        y_bf = {}
        sums = {}
        passes = {}

        on_scalar = nc.scalar.copy
        on_vector = nc.vector.tensor_copy

        def load_scale_rows(tile, rows, count):
            for q in range(QUADS):
                nc.sync.dma_start(
                    tile[32 * q : 32 * q + SCALE_ROWS * count, :].bitcast(I32),
                    rows[:, SCALE_ROWS * q : SCALE_ROWS * (q + 1), :].bitcast(I32),
                )

        def load_state(a, t):
            state[a, t] = rows_tile("state%d_%d" % (a, t))
            rows = gT[GROUP * a : GROUP * (a + 1), :].rearrange("(p t) w -> p t w", t=PACK)
            nc.sync.dma_start(state[a, t][:], rows[:, t, :])

        def load_wc(c0):
            cols = slice(c0, c0 + wc_raw[c0].shape[2])
            nc.sync.dma_start(wc_raw[c0][:], wc[:, cols].rearrange("(p j) n -> p j n", j=PACK))

        def load_uc(a):
            nc.sync.dma_start(uc_raw[a][:], uc_words[a].rearrange("p e i -> p (e i)").bitcast(I32))

        def deal_narrow(dst, src, size, copy=on_vector):
            copy(
                out=dst.rearrange("p (t c i) -> p c t i", t=PACK, i=LINE // size),
                in_=src.rearrange("p (c i t) -> p c t i", t=PACK, i=LINE // size),
            )

        def deal_uc(a):
            nc.scalar.copy(
                out=uc_w[a][:].rearrange("p (t m) -> p m t", t=PACK),
                in_=uc_raw[a][:].bitcast(U32).rearrange("p (m t) -> p m t", t=PACK),
            )

        def picks(j0, n):
            return offsets[:, j0 // 16 : (j0 + n) // 16]

        def dealt(g, t):
            return slice(t * (H // PACK) + g * P, t * (H // PACK) + (g + 1) * P)

        def planes(rows, j0, n):
            return rows[:].rearrange("p (t w) -> p t w", t=PACK)[:, :, j0 : j0 + n]

        def gates(a, t, j0, n):
            first = max(j for group, plane, j in gate if (group, plane) == (a, t) and j <= j0)
            return gate[a, t, first][:, j0 - first : j0 - first + n]

        def make_gate(a, t, j0):
            acc = psum.tile([P, BANK], F32, name="acc")
            cols = dealt(a, t)
            nc.tensor.matmul_mx(
                out=acc[:],
                lhsT=wr_w[:, 2 * cols.start : 2 * cols.stop].bitcast(FP4X4),
                lhsT_scale=wr_s[a][:, t * P : (t + 1) * P],
                rhs=v_w[j0][:].bitcast(FP8X4),
                rhs_scale=v_s[:, j0 : j0 + BANK],
                start=True,
                stop=True,
            )
            cuts = [j0] + [j for group, plane, j in sorted(gate) if (group, plane) == (a, t) and j0 < j < j0 + BANK]
            for c0, c1 in zip(cuts, cuts[1:] + [j0 + BANK]):
                nc.scalar.activation(out=gates(a, t, c0, c1 - c0), in_=acc[:, c0 - j0 : c1 - j0], func=ACT.Sigmoid)

        def gather_state(a, t, j0, n):
            nc.vector.tensor_tensor(
                planes(h_rows[a], j0, n)[:, t, :],
                state[a, t][:].indirect(picks(j0, n)),
                gates(a, t, j0, n),
                MULT,
            )

        def weave(copy, woven, planar, some=slice(0, PACK)):
            copy(
                out=woven.rearrange("p (c i t) -> p c t i", t=PACK, i=PAIR)[:, :, some, :],
                in_=planar.rearrange("p t (c i) -> p c t i", i=PAIR)[:, :, some, :],
            )

        def woven_h(a, j0, n):
            first = max(j for group, j in h_bf if group == a and j <= j0)
            return h_bf[a, first][:, PACK * (j0 - first) : PACK * (j0 - first + n)]

        def weave_h(a, j0, n, copy, some=slice(0, PACK)):
            weave(copy, woven_h(a, j0, n), planes(h_rows[a], j0, n), some)

        def quantise_h(a, j0, n):
            nc.vector.quantize_mx(
                out=h_w[a][:, j0 : j0 + n].bitcast(FP8X4),
                scales=h_s[a][:, j0 : j0 + n],
                in_=woven_h(a, j0, n),
            )

        def weave_wc(c0):
            m0, count = c0 % GROUP // PACK, wc_raw[c0].shape[2] // PACK
            nc.scalar.copy(
                out=wc_bf[c0 // GROUP][:].rearrange("p (t m j) -> p m j t", t=PACK, j=PACK)[:, m0 : m0 + count],
                in_=wc_raw[c0][:].rearrange("p j (m t) -> p m j t", t=PACK),
            )

        def quantise_wc(g, c0, n):
            cols = slice(c0, c0 + n)
            woven = wc_bf[g][:, PACK * c0 : PACK * (c0 + n)]
            nc.vector.quantize_mx(out=wc_w[g][:, cols].bitcast(FP8X4), scales=wc_s[g][:, cols], in_=woven)

        def add_pass(g, j0, t, term):
            done = passes.setdefault((g, j0, t), [])
            if not done:
                sums[g, j0, t] = psum.tile([P, BANK], F32, name="acc")
            done.append(term)
            cols = slice(j0, j0 + BANK)
            if term == TOKEN:
                own = slice(t * P, (t + 1) * P)
                w, w_scale = wc_w[g][:, own], wc_s[g][:, own]
                x, x_scale = v_w[j0][:], v_s[:, cols]
            else:
                w, w_scale = uc_w[term][:, dealt(g, t)], uc_s[SCALE_ROWS * term :, dealt(g, t)]
                x, x_scale = h_w[term][:, cols], h_s[term][:, cols]
            nc.tensor.matmul_mx(
                out=sums[g, j0, t][:],
                lhsT=w.bitcast(FP8X4),
                lhsT_scale=w_scale,
                rhs=x.bitcast(FP8X4),
                rhs_scale=x_scale,
                start=(len(done) == 1),
                stop=(len(done) == PASSES),
            )

        def open_sums(g, j0, term):
            for t in range(PACK):
                add_pass(g, j0, t, term)

        def make_y(g, j0, terms, scalar_gains, apart=None, plane=PACK - 2):
            y_rows[g, j0] = rows_tile("y%d_%d" % (g, j0))
            y = planes(y_rows[g, j0], 0, BANK)
            rows = out_0[GROUP * g : GROUP * (g + 1), j0 : j0 + BANK].rearrange("(p t) j -> p t j", t=PACK)
            tanh = [y[:, t, :] for t in range(PACK)]
            if apart is not None:
                tanh[plane] = apart
            for pair in range(0, PACK, 2):
                for t in (pair, pair + 1):
                    for term in terms:
                        add_pass(g, j0, t, term)
                    nc.scalar.activation(
                        out=tanh[t], in_=sums[g, j0, t][:], func=ACT.Tanh, bias=bias[:, g, t : t + 1]
                    )
                for t in (pair, pair + 1):
                    row = y[:, t, :]
                    if t < scalar_gains:
                        nc.scalar.activation(out=row, in_=row, func=ACT.Copy, scale=gains[:, g, t : t + 1])
                    else:
                        nc.vector.tensor_scalar(out=row, in0=tanh[t], scalar1=gains[:, g, t : t + 1], scalar2=None, op0=MULT)
                nc.sync.dma_start(rows[:, pair : pair + 2, :], y[:, pair : pair + 2, :])

        def weave_y(g, j0, c0, n, copy):
            if (g, j0) not in y_bf:
                y_bf[g, j0] = kept("y_bf%d_%d" % (g, j0), PACK * BANK, BF16, ("wc_raw512", "wc_bf0", "gate0_0", "gate0_1")[len(y_bf)])
            weave(copy, y_bf[g, j0][:, PACK * c0 : PACK * (c0 + n)], planes(y_rows[g, j0], c0, n))

        def quantise_y(g, j0):
            cols = slice(j0, j0 + BANK)
            nc.vector.quantize_mx(
                out=y_w[g][:, cols].bitcast(FP8X4), scales=y_s[SCALE_ROWS * g :, cols], in_=y_bf[g, j0][:]
            )

        def store_words(g, j0, n):
            nc.sync.dma_start(
                out_1[g, :, j0 : j0 + n, :].rearrange("p m t -> p (m t)").bitcast(I32),
                y_w[g][:, j0 : j0 + n].bitcast(I32),
            )

        nc.vector.memset(tab_s[:].bitcast(I32), 0)
        nc.vector.memset(wr_s_raw[:].bitcast(I32), 0)
        nc.vector.memset(uc_s_raw[:].bitcast(I32), 0)
        warm = keep.tile([P, 2], F32, name="warm")
        nc.vector.memset(warm[:], 0.0)
        nc.scalar.activation(out=warm[:, 1:2], in_=warm[:, 0:1], func=ACT.Sigmoid)

        nc.sync.dma_start(offsets[:], offs)
        nc.sync.dma_start(wr_raw[:].bitcast(I32), wr_words[0].bitcast(I32))
        load_scale_rows(tab_s, tab_scales, 1)
        nc.sync.dma_start(tab_w[:], tab_words[0].rearrange("p t i -> p (t i)").bitcast(I32))
        load_scale_rows(wr_s_raw, wr_scales, 1)
        for t in range(PACK - 1):
            load_state(0, t)
        load_uc(0)
        load_state(0, PACK - 1)
        load_state(1, 0)
        load_state(1, 1)
        load_scale_rows(uc_s_raw, uc_scales, GROUPS)
        load_wc(0)
        load_state(1, 2)
        load_state(1, 3)
        load_uc(1)
        load_wc(GROUP)
        load_wc(GROUP + QUARTER)
        nc.sync.dma_start(bias[:], b.rearrange("(g p t) -> p g t", p=P, t=PACK))
        nc.sync.dma_start(gains[:], gain.rearrange("(g p t) -> p g t", p=P, t=PACK))

        deal_narrow(wr_w[:].bitcast(U16), wr_raw[:].bitcast(U16), 2)
        nc.vector.tensor_copy(v_s[:], tab_s[:].indirect(offsets[:]))
        v_w[0] = kept("v_w0", BANK, U32)
        nc.vector.tensor_copy(v_w[0][:], tab_w[:].bitcast(U32).indirect(picks(0, BANK)))
        for a in range(GROUPS):
            deal_narrow(wr_s[a][:], wr_s_raw[:, GROUP * a : GROUP * (a + 1)], 1, nc.gpsimd.tensor_copy)
        v_w[BANK] = kept("v_w1", BANK, U32)
        nc.vector.tensor_copy(v_w[BANK][:], tab_w[:].bitcast(U32).indirect(picks(BANK, BANK)))

        for a in range(GROUPS):
            for t in range(PACK):
                for j0 in (0, BANK):
                    make_gate(a, t, j0)

        for t in range(PACK):
            width = BANK if t == 0 else S
            for j0 in range(0, S, width):
                gather_state(0, t, j0, width)
        gather_state(1, 0, 0, S)
        for t, end in ((1, S), (2, FIRST)):
            gather_state(1, t, 0, BANK)
            gather_state(1, t, BANK, end - BANK)
        deal_uc(0)
        weave_h(0, 0, S, on_scalar)
        deal_narrow(uc_s[:], uc_s_raw[:], 1)
        h_w[0] = kept("h_w0", S, U32, "gate1_1_0")
        quantise_h(0, 0, S)
        weave_wc(0)
        wc_w[0] = kept("wc_w0", GROUP, U32, "gate1_2_0")
        quantise_wc(0, 0, GROUP)
        h_bf[1, 0] = kept("h_bf1", PACK * BANK, BF16, "wc_raw0")
        weave_h(1, 0, BANK, on_scalar, slice(0, 2))
        deal_uc(1)
        open_sums(0, 0, 0)
        open_sums(0, 0, TOKEN)
        open_sums(1, 0, 0)

        last = PACK - 1
        for step in (lambda j0: gather_state(1, last, j0, SLICE), lambda j0: weave_h(1, j0, SLICE, on_vector, slice(2, PACK)), lambda j0: quantise_h(1, j0, SLICE)):
            for j0 in range(0, BANK, SLICE):
                step(j0)
        weave_wc(GROUP)
        weave_wc(GROUP + QUARTER)
        for c0 in (0, QUARTER):
            quantise_wc(1, c0, QUARTER)
        gather_state(1, last, BANK, BANK)
        gather_state(1, 2, FIRST, S - FIRST)
        h_bf[1, BANK] = wc_bf[1]
        for j0 in (BANK, BANK + SLICE):
            weave_h(1, j0, SLICE, on_vector)
        for j0 in (BANK, BANK + SLICE):
            quantise_h(1, j0, SLICE)
        make_y(0, 0, (1,), 2)
        y_bf[0, 0] = kept("y_bf0_0", PACK * BANK, BF16, "gate0_2")
        weave_y(0, 0, 0, SLICE, on_vector)
        make_y(1, 0, (1, TOKEN), 0, y_bf[0, 0][:, PACK * SLICE :].bitcast(F32), 1)
        weave_y(0, 0, SLICE, SLICE, on_vector)
        y_bf[1, 0] = kept("y_bf1_0", PACK * BANK, BF16, "wc_bf0")
        weave_y(1, 0, 0, SLICE, on_vector)
        make_y(0, BANK, (0, TOKEN, 1), 0, y_bf[1, 0][:, PACK * SLICE :].bitcast(F32), 1)
        make_y(1, BANK, (0, TOKEN, 1), 0)

        weave_y(1, 0, SLICE, SLICE, on_vector)
        for g in range(GROUPS):
            quantise_y(g, 0)
            store_words(g, 0, BANK)
        weave_y(0, BANK, 0, SLICE, on_vector)
        weave_y(0, BANK, SLICE, SLICE, on_scalar)
        weave_y(1, BANK, 0, SHARE, on_scalar)
        weave_y(1, BANK, SHARE, BANK - SHARE, on_vector)
        for g in range(GROUPS):
            quantise_y(g, BANK)
            store_words(g, BANK, BANK)
        for q in range(QUADS):
            nc.scalar.dma_start(
                out_2[:, SCALE_ROWS * q : SCALE_ROWS * (q + 1), :].bitcast(I32),
                y_s[32 * q : 32 * q + SCALE_ROWS * GROUPS, :].bitcast(I32),
            )
